import numpy as np
import ml_dtypes


def mxq(x, axis, fmt="e4m3"):
    dtype, down = {"e4m3": (ml_dtypes.float8_e4m3fn, 7), "e5m2": (ml_dtypes.float8_e5m2, 14)}[fmt]
    v = np.moveaxis(np.asarray(x, np.float32).astype(ml_dtypes.bfloat16).astype(np.float64), axis, -1)
    blocks = v.reshape(v.shape[:-1] + (-1, 32))
    amax = np.abs(blocks).max(-1, keepdims=True)
    byte = np.maximum(np.where(amax > 0, np.frexp(amax)[1] - 1 + 127, 0) - down, 1)
    scale = np.exp2(byte - 127.0)
    codes = (blocks / scale).astype(np.float32).astype(dtype).astype(np.float64)
    return np.moveaxis((codes * scale).reshape(v.shape), -1, axis)


WIDE = False


def mx_kscale(k):
    if not WIDE:
        return np.ones(k)
    levels = np.array([10, -10, 5, -5, 0])
    if k % 512:
        return np.exp2(np.random.permutation(np.resize(levels, k // 32))).repeat(32)
    a = np.empty((k // 512, 16))
    for p in range(k // 512):
        a[p, :8] = np.random.permutation(np.resize(levels, 8))
        for g in range(8):
            far = levels[np.abs(levels - a[p, g]) >= 10]
            a[p, g + 8] = far[np.random.randint(len(far))]
    return np.exp2(a.ravel()).repeat(32)


def f64(x):
    return np.asarray(x).astype(np.float64)


def striped(idx):
    return np.tile(idx.reshape(-1, 16).T, (8, 1)).astype(np.uint16)


def unstriped(offs):
    return offs[:16].T.reshape(-1).astype(np.int64)


E2M1 = np.array([0.0, 0.5, 1.0, 1.5, 2.0, 3.0, 4.0, 6.0, -0.0, -0.5, -1.0, -1.5, -2.0, -3.0, -4.0, -6.0])


def pack_weight(w, fmt):
    k, n = w.shape
    w = f64(np.asarray(w, np.float32).astype(ml_dtypes.bfloat16)).reshape(k // 32, 32, n)
    amax = np.abs(w).max(1)
    if fmt == "e4m3":
        byte = np.frexp(amax)[1] - 1 + 127 - 7
    else:
        mant, ex = np.frexp(amax / 6.0)
        byte = np.where(mant > 0.5, ex, ex - 1) + 127
    byte = np.clip(np.where(amax > 0, byte, 1), 1, 254)
    scaled = (w * np.exp2(127.0 - byte)[:, None, :]).reshape(k, n).astype(np.float32)
    by_word = np.ascontiguousarray(scaled.reshape(k // 512, 128, 4, n).transpose(0, 1, 3, 2))
    if fmt == "e4m3":
        words = by_word.astype(ml_dtypes.float8_e4m3fn).view(np.uint8)
    else:
        c = by_word.astype(ml_dtypes.float4_e2m1fn).view(np.uint8) & 0xF
        words = (c[..., 0::2] | (c[..., 1::2] << 4)).reshape(k // 512, 128, 2 * n)
    return np.ascontiguousarray(words), np.ascontiguousarray(byte.astype(np.uint8).reshape(k // 512, 16, n))


def unpack_weight(words, scales, fmt):
    g, _, n = scales.shape
    words = np.ascontiguousarray(words).reshape(g, 128, n, -1)
    if fmt == "e4m3":
        vals = words.view(ml_dtypes.float8_e4m3fn).astype(np.float64)
    else:
        nib = np.empty((g, 128, n, 4), np.uint8)
        nib[..., 0::2] = words & 0xF
        nib[..., 1::2] = words >> 4
        vals = E2M1[nib]
    vals = vals * np.repeat(np.exp2(scales.astype(np.float64) - 127.0), 8, axis=1)[..., None]
    return vals.transpose(0, 1, 3, 2).reshape(g * 512, n)


def gelu(v):
    return 0.5 * v * (1.0 + np.tanh(np.sqrt(2.0 / np.pi) * (v + 0.044715 * v**3)))


K, T, S, T2, T3, S2, P = 1024, 2048, 512, 1024, 2048, 512, 512


def setup_inputs():
    n = np.random.standard_normal
    s = mx_kscale(K)[:, None]
    tab_words, tab_scales = pack_weight(n((K, T)) * s, "e4m3")
    w4_words, w4_scales = pack_weight(n((K, K)) / np.sqrt(K) / s * s.T, "e2m1")
    tab2_words, tab2_scales = pack_weight(n((K, T3)) / np.sqrt(K) / s, "e4m3")
    return {
        "tab_words": tab_words, "tab_scales": tab_scales,
        "offs": striped(np.random.permutation(T)[:S]),
        "w1": (n((K, K)) / np.sqrt(K) / s * s.T).astype(np.float32),
        "w4_words": w4_words, "w4_scales": w4_scales,
        "page0": (n((K, T2)) * s).astype(np.float32),
        "wgs": np.exp(0.3 * n((128, S))).astype(np.float32),
        "offs3": striped(np.random.permutation(T2)[:S]),
        "tab2_words": tab2_words, "tab2_scales": tab2_scales,
        "offs2": striped(np.random.permutation(T3)[:S2]),
        "offs4": striped(np.random.permutation(T2)[:P]),
        "be": np.random.uniform(0.4, 1.2, S2).astype(np.float32),
        "ref": n((S2, P)).astype(np.float32),
    }


def reference(tab_words, tab_scales, offs, w1, w4_words, w4_scales, page0, wgs, offs3,
              tab2_words, tab2_scales, offs2, offs4, be, ref):
    v = unpack_weight(tab_words, tab_scales, "e4m3")[:, unstriped(offs)]
    b = mxq(f64(w1), 0, "e4m3")
    a = unpack_weight(w4_words, w4_scales, "e2m1")
    p = mxq(np.maximum(b.T @ v, 0.0), 0, "e4m3")
    q = mxq(np.maximum(a.T @ v, 0.0), 0, "e4m3")
    h = (a.T @ p) - (b.T @ q)
    page = f64(page0).copy()
    page[:, unstriped(offs3)] = np.tile(f64(wgs), (K // 128, 1)) * h
    v2 = unpack_weight(tab2_words, tab2_scales, "e4m3")[:, unstriped(offs2)]
    e = v2.T @ mxq(page, 0, "e4m3")
    return e[:, unstriped(offs4)] + f64(be)[:, None] * f64(ref)

@@ -1,0 +1,358 @@
+from contextlib import ExitStack
+
+import concourse.mybir as mybir
+
+K, T, S, T2, T3, S2, PICK = 1024, 2048, 512, 1024, 2048, 512, 512
+FLOPS = 4 * 2 * K * K * S + 2 * K * S2 * T2
+
+F32 = mybir.dt.float32
+BF16 = mybir.dt.bfloat16
+I32 = mybir.dt.int32
+U32 = mybir.dt.uint32
+U16 = mybir.dt.uint16
+U8 = mybir.dt.uint8
+FP8X4 = mybir.dt.float8_e4m3fn_x4
+FP4X4 = mybir.dt.float4_e2m1fn_x4
+MULT = mybir.AluOpType.mult
+ADD = mybir.AluOpType.add
+MAX = mybir.AluOpType.max
+RELU = mybir.ActivationFunctionType.Relu
+COPY = mybir.ActivationFunctionType.Copy
+
+P = 128
+PACK = 4
+PASS = P * PACK
+PASSES = K // PASS
+BANK = 512
+CHUNK = 128
+ALIGN = 64
+
+
+def tile_list_binning_order_scores_kernel(
+    tc, tab_words, tab_scales, offs, w1, w4_words, w4_scales, page0, wgs, offs3,
+    tab2_words, tab2_scales, offs2, offs4, be, ref, out,
+):
+    nc = tc.nc
+    with ExitStack() as ctx:
+        lists = ctx.enter_context(tc.tile_pool(name="lists", bufs=1))
+        keep = ctx.enter_context(tc.tile_pool(name="keep", bufs=1))
+        ring = ctx.enter_context(tc.tile_pool(name="ring", bufs=4))
+        psum = ctx.enter_context(tc.psum_pool(name="psum", bufs=8))
+
+        def held(name, shape, dtype):
+            return keep.tile(shape, dtype, name=name, align_bytes=ALIGN)
+
+        def bank(name):
+            return psum.tile([P, BANK], F32, name=name, tag="bank")
+
+        idx = lists.tile([P, S // 16], U16, name="idx")
+        idx2 = lists.tile([P, S2 // 16], U16, name="idx2")
+        idx3 = lists.tile([P, S // 16], U16, name="idx3")
+        idx4 = lists.tile([P, PICK // 16], U16, name="idx4")
+
+        w4_scale_raw = held("w4_scale_raw", [P, PASSES, K], U8)
+        tab_scale = held("tab_scale", [P, PASSES, T], U8)
+        tab2_scale = held("tab2_scale", [P, T3], U8)
+        nc.vector.memset(tab_scale[:, 0, :].bitcast(I32), 0)
+        nc.gpsimd.memset(tab_scale[:, 1, :].bitcast(I32), 0)
+        nc.vector.memset(w4_scale_raw[:].rearrange("p a c -> p (a c)").bitcast(I32), 0)
+        nc.vector.memset(tab2_scale[:].bitcast(I32), 0)
+
+        w4_raw = held("w4_raw", [P, PASSES, K // 2], I32)
+        tab_word = [held("tab_word%d" % a, [P, T], I32) for a in range(PASSES)]
+        nc.sync.dma_start(w4_raw[:], w4_words.bitcast(I32).rearrange("a p w -> p a w"))
+        nc.sync.dma_start(idx[:], offs)
+
+        def load_scales(plane, rows_in):
+            for quad in range(4):
+                nc.sync.dma_start(
+                    plane[32 * quad : 32 * quad + 4].bitcast(I32),
+                    rows_in[:, 4 * quad : 4 * quad + 4, :].bitcast(I32).rearrange("a r w -> r a w"),
+                )
+
+        load_scales(tab_scale, tab_scales)
+        nc.sync.dma_start(tab_word[0][:], tab_words[0].rearrange("p n i -> p (n i)").bitcast(I32))
+        load_scales(w4_scale_raw, w4_scales)
+        nc.sync.dma_start(tab_word[1][:], tab_words[1].rearrange("p n i -> p (n i)").bitcast(I32))
+
+        w1_raw = {}
+        for b in range(PASSES):
+            for a in range(PASSES):
+                w1_raw[a, b] = ring.tile([P, PACK, PASS], F32, name="w1_raw", tag="wide", align_bytes=ALIGN)
+                nc.sync.dma_start(
+                    w1_raw[a, b][:],
+                    w1[PASS * a : PASS * (a + 1), PASS * b : PASS * (b + 1)].rearrange("(p i) c -> p i c", i=PACK),
+                )
+
+        nc.sync.dma_start(idx3[:], offs3)
+        gain = [held("gain%d" % u, [P, 2, S], F32) for u in range(2)]
+        page = {(a, t): held("page%d%d" % (a, t), [P, T2], F32) for a in range(PASSES) for t in range(PACK)}
+        wgs_rows = wgs.rearrange("(m t) j -> m t j", t=PACK)
+        page_rows = page0.rearrange("(a p t) c -> a t p c", a=PASSES, t=PACK)
+
+        def load_gain(u):
+            for quad in range(4):
+                nc.sync.dma_start(gain[u][32 * quad : 32 * quad + 32], wgs_rows[:, 2 * u : 2 * u + 2, :])
+
+        for u in range(2):
+            load_gain(u)
+            for t in (2 * u, 2 * u + 1):
+                nc.sync.dma_start(page[0, t][:], page_rows[0, t])
+
+        nc.sync.dma_start(idx2[:], offs2)
+        for quad in range(4):
+            nc.sync.dma_start(
+                tab2_scale[32 * quad : 32 * quad + 8].bitcast(I32),
+                tab2_scales[:, 4 * quad : 4 * quad + 4, :].bitcast(I32),
+            )
+        tab2_word = [held("tab2_word%d" % a, [P, T3], I32) for a in range(PASSES)]
+        for a in range(PASSES):
+            nc.sync.dma_start(tab2_word[a][:], tab2_words[a].rearrange("p n i -> p (n i)").bitcast(I32))
+        nc.sync.dma_start(idx4[:], offs4)
+        blend = held("blend", [P, S2 // P], F32)
+        with nc.allow_non_contiguous_dma(reason="one weight to a partition"):
+            nc.sync.dma_start(blend[:], be.rearrange("(i p) -> p i", p=P))
+        prior = held("prior", [P, S2 // P, PICK], F32)
+        nc.sync.dma_start(prior[:], ref.rearrange("(i p) m -> p i m", p=P))
+        for t in range(PACK):
+            nc.sync.dma_start(page[1, t][:], page_rows[1, t])
+
+        w4_code = [held("w4_code%d" % a, [P, 2 * K], U8) for a in range(PASSES)]
+        w4_scale = [held("w4_scale%d" % a, [P, K], U8) for a in range(PASSES)]
+        v_code = [held("v_code%d" % a, [P, S], I32) for a in range(PASSES)]
+        v_scale = [held("v_scale%d" % a, [P, S], U8) for a in range(PASSES)]
+
+        def order_words(a):
+            nc.vector.tensor_copy(
+                w4_code[a][:].bitcast(U16).rearrange("p (b t m) -> p b t m", b=PASSES, t=PACK),
+                w4_raw[:, a, :].bitcast(U16).rearrange("p (b m t) -> p b t m", b=PASSES, t=PACK),
+            )
+
+        def order_scales(a):
+            nc.vector.tensor_copy(
+                w4_scale[a][:].rearrange("p (b t m) -> p b t m", b=PASSES, t=PACK),
+                w4_scale_raw[:, a, :].rearrange("p (b m t) -> p b t m", b=PASSES, t=PACK),
+            )
+
+        for a in range(PASSES):
+            order_words(a)
+            nc.vector.tensor_copy(v_code[a][:].bitcast(U32), tab_word[a][:].bitcast(U32).indirect(idx[:]))
+            order_scales(a)
+            nc.vector.tensor_copy(v_scale[a][:], tab_scale[:, a, :].indirect(idx[:]))
+
+        w1_code, w1_scale = {}, {}
+
+        def w4_side(a, b, t):
+            c = PASS * b + P * t
+            return w4_code[a][:, 2 * c : 2 * (c + P)].bitcast(FP4X4), w4_scale[a][:, c : c + P]
+
+        def w1_side(a, b, t):
+            c = P * t
+            return w1_code[a, b][:, c : c + P].bitcast(FP8X4), w1_scale[a, b][:, c : c + P]
+
+        def mx(acc, side, code, scale, cols, start, stop):
+            nc.tensor.matmul_mx(
+                out=acc, lhsT=side[0], lhsT_scale=side[1],
+                rhs=code[:, cols].bitcast(FP8X4), rhs_scale=scale[:, cols], start=start, stop=stop,
+            )
+
+        def first_stage_pass(acc, side_of, a, b, c):
+            cols = slice(CHUNK * c, CHUNK * (c + 1))
+            for t in range(PACK):
+                mx(acc[:, CHUNK * t : CHUNK * (t + 1)], side_of(a, b, t), v_code[a], v_scale[a], cols,
+                   a == 0 and t == 0, a == PASSES - 1 and t == PACK - 1)
+
+        def rectify(dst, acc, c, sign, on_vector):
+            woven = dst[:, PACK * CHUNK * c : PACK * CHUNK * (c + 1)].rearrange("p (n t) -> p n t", t=PACK)
+            src = acc[:].rearrange("p (t n) -> p n t", t=PACK)
+            if on_vector:
+                nc.vector.tensor_scalar(woven, src, sign, 0.0, MULT, MAX)
+            else:
+                nc.scalar.activation(woven, src, RELU, scale=sign)
+
+        def quantize(code, scale, src, lo, hi):
+            nc.vector.quantize_mx(code[:, lo:hi].bitcast(FP8X4), scale[:, lo:hi], src[:, PACK * lo : PACK * hi])
+
+        def prepare_w1(a, b, split):
+            rounded = ring.tile([P, PACK * PASS], BF16, name="w1_bf", tag="mid", align_bytes=ALIGN)
+            dst = rounded[:].rearrange("p (t m i) -> p m t i", t=PACK, i=PACK)
+            src = w1_raw[a, b][:].rearrange("p i (m t) -> p m t i", t=PACK)
+            nc.vector.tensor_scalar(dst[:, :split], src[:, :split], -1.0, None, MULT)
+            if split < P:
+                nc.scalar.activation(dst[:, split:], src[:, split:], COPY, scale=-1.0)
+            w1_code[a, b] = held("w1_code%d%d" % (a, b), [P, PASS], I32)
+            w1_scale[a, b] = held("w1_scale%d%d" % (a, b), [P, PASS], U8)
+            quantize(w1_code[a, b], w1_scale[a, b], rounded, 0, PASS)
+
+        chunks = S // CHUNK
+        q_bf = [held("q_bf%d" % b, [P, PACK * S], BF16) for b in range(PASSES)]
+        p_bf = [held("p_bf%d" % b, [P, PACK * S], BF16) for b in range(PASSES)]
+        q_code = [held("q_code%d" % b, [P, S], I32) for b in range(PASSES)]
+        p_code = [held("p_code%d" % b, [P, S], I32) for b in range(PASSES)]
+        q_scale = [held("q_scale%d" % b, [P, S], U8) for b in range(PASSES)]
+        p_scale = [held("p_scale%d" % b, [P, S], U8) for b in range(PASSES)]
+
+        q_acc = {(b, c): bank("q_acc") for b in range(PASSES) for c in range(chunks)}
+        for a in range(PASSES):
+            for b in range(PASSES):
+                for c in range(chunks):
+                    first_stage_pass(q_acc[b, c], w4_side, a, b, c)
+        prepare_w1(0, 0, 96)
+        for c in range(chunks):
+            rectify(q_bf[0], q_acc[0, c], c, 1.0, False)
+        prepare_w1(1, 0, P)
+        for c in range(chunks):
+            rectify(q_bf[1], q_acc[1, c], c, 1.0, False)
+        quantize(q_code[0], q_scale[0], q_bf[0], 0, S)
+
+        p_acc = {(b, c): bank("p_acc") for b in range(PASSES) for c in range(chunks)}
+        for a in range(PASSES):
+            for c in range(chunks):
+                first_stage_pass(p_acc[0, c], w1_side, a, 0, c)
+        prepare_w1(0, 1, P)
+        quantize(q_code[1], q_scale[1], q_bf[1], 0, S)
+        for c in range(chunks):
+            rectify(p_bf[0], p_acc[0, c], c, -1.0, False)
+        for c in range(chunks):
+            first_stage_pass(p_acc[1, c], w1_side, 0, 1, c)
+        prepare_w1(1, 1, 88)
+        quantize(p_code[0], p_scale[0], p_bf[0], 0, S)
+
+        half = S // 2
+        head_acc = [bank("head_acc") for u in range(2)]
+
+        def head_q(u):
+            cols = slice(half * u, half * (u + 1))
+            for a in range(PASSES):
+                for t in range(2):
+                    mx(head_acc[u][:, half * t : half * (t + 1)], w1_side(a, 0, t), q_code[a], q_scale[a], cols,
+                       a == 0 and t == 0, False)
+
+        def head_p(u, a):
+            for t in range(2):
+                for c in range(2):
+                    lo = half * u + CHUNK * c
+                    at = half * t + CHUNK * c
+                    mx(head_acc[u][:, at : at + CHUNK], w4_side(a, 0, t), p_code[a], p_scale[a],
+                       slice(lo, lo + CHUNK), False, a == PASSES - 1 and t == 1 and c == 1)
+
+        for c in range(2):
+            first_stage_pass(p_acc[1, c], w1_side, 1, 1, c)
+        head_q(0)
+        head_p(0, 0)
+        for c in range(2, chunks):
+            first_stage_pass(p_acc[1, c], w1_side, 1, 1, c)
+
+        rectify(p_bf[1], p_acc[1, 0], 0, -1.0, False)
+        rectify(p_bf[1], p_acc[1, 1], 1, -1.0, True)
+        quantize(p_code[1], p_scale[1], p_bf[1], 0, half)
+        rectify(p_bf[1], p_acc[1, 2], 2, -1.0, False)
+        head_p(0, 1)
+        head_sb = [held("head_sb%d" % u, [P, 2, half], F32) for u in range(2)]
+        nc.scalar.copy(head_sb[0][:].rearrange("p t j -> p (t j)"), head_acc[0][:])
+        rectify(p_bf[1], p_acc[1, 3], 3, -1.0, False)
+
+        def scatter(a, t, src, lo, hi):
+            nc.vector.tensor_tensor(
+                page[a, t][:].indirect(idx3[:, lo // 16 : hi // 16]), src, gain[t // 2][:, t % 2, lo:hi], MULT
+            )
+
+        scatter(0, 0, head_sb[0][:, 0, :], 0, half)
+        quantize(p_code[1], p_scale[1], p_bf[1], half, S)
+        scatter(0, 1, head_sb[0][:, 1, :], 0, half)
+        head_q(1)
+        head_p(1, 0)
+        head_p(1, 1)
+        nc.scalar.copy(head_sb[1][:].rearrange("p t j -> p (t j)"), head_acc[1][:])
+
+        h_sb = {}
+        whole = slice(0, S)
+        rest = [(0, 2), (0, 3)] + [(1, t) for t in range(PACK)]
+        for b, t in rest:
+            acc = bank("h_acc")
+            for a in range(PASSES):
+                mx(acc[:], w1_side(a, b, t), q_code[a], q_scale[a], whole, a == 0, False)
+            for a in range(PASSES):
+                mx(acc[:], w4_side(a, b, t), p_code[a], p_scale[a], whole, False, a == PASSES - 1)
+            h_sb[b, t] = keep.tile([P, S], F32, name="h_sb", tag="h_sb%d%d" % (b, t), align_bytes=ALIGN)
+            nc.scalar.copy(h_sb[b, t][:], acc[:])
+
+        planes = [ring.tile([P, PACK, T2], BF16, name="planes", tag="wide", align_bytes=ALIGN) for a in range(PASSES)]
+        woven = [ring.tile([P, PACK * T2], BF16, name="woven", tag="wide", align_bytes=ALIGN) for a in range(PASSES)]
+        page_code = [held("page_code%d" % a, [P, T2], I32) for a in range(PASSES)]
+        page_scale = [None, held("page_scale1", [P, T2], U8)]
+
+        def round_plane(a, t, lo, hi, copy):
+            copy(planes[a][:, t, lo:hi], page[a, t][:, lo:hi])
+
+        def weave(a, lo, hi, copy):
+            copy(
+                woven[a][:, PACK * lo : PACK * hi].rearrange("p (c i t) -> p c t i", i=4, t=PACK),
+                planes[a][:, :, lo:hi].rearrange("p t (c i) -> p c t i", i=4),
+            )
+
+        for t in range(2):
+            scatter(0, t, head_sb[1][:, t, :], half, S)
+            round_plane(0, t, 0, T2, nc.scalar.copy)
+        for t in range(2, PACK):
+            scatter(0, t, h_sb[0, t][:], 0, S)
+            round_plane(0, t, 0, T2, nc.scalar.copy)
+        for u in range(2):
+            weave(0, BANK * u, BANK * (u + 1), nc.scalar.copy)
+
+        v2_code = [held("v2_code%d" % a, [P, S2], I32) for a in range(PASSES)]
+        v2_scale = held("v2_scale", [P, S2], U8)
+        nc.vector.tensor_copy(v2_scale[:], tab2_scale[:].indirect(idx2[:]))
+        for a in range(PASSES):
+            nc.vector.tensor_copy(v2_code[a][:].bitcast(U32), tab2_word[a][:].bitcast(U32).indirect(idx2[:]))
+
+        rows = S2 // P
+        e_acc = {}
+
+        def score_pass(a, i, u):
+            side = (v2_code[a][:, P * i : P * (i + 1)].bitcast(FP8X4), v2_scale[4 * a :, P * i : P * (i + 1)])
+            mx(e_acc[i, u][:], side, page_code[a], page_scale[a], slice(BANK * u, BANK * (u + 1)), a == 0, a == 1)
+
+        scatter(1, 0, h_sb[1, 0][:], 0, S)
+        round_plane(1, 0, 0, T2, nc.scalar.copy)
+        scatter(1, 1, h_sb[1, 1][:], 0, S)
+        round_plane(1, 1, 0, T2, nc.scalar.copy)
+        for i in range(rows):
+            nc.scalar.activation(prior[:, i, :], prior[:, i, :], COPY, scale=blend[:, i : i + 1])
+        scatter(1, 2, h_sb[1, 2][:], 0, S)
+        round_plane(1, 2, 0, T2, nc.scalar.copy)
+        page_scale[0] = keep.tile([P, T2], U8, name="page_scale0", tag="h_sb12", align_bytes=ALIGN)
+        quantize(page_code[0], page_scale[0], woven[0], 0, T2)
+        for u in range(2):
+            for i in range(rows):
+                e_acc[i, u] = bank("e_acc")
+                score_pass(0, i, u)
+        scatter(1, 3, h_sb[1, 3][:], 0, S)
+
+        cut = 896
+        round_plane(1, 3, 0, BANK, nc.vector.tensor_copy)
+        round_plane(1, 3, BANK, T2, nc.scalar.copy)
+        weave(1, BANK, cut, nc.scalar.copy)
+        weave(1, 0, BANK, nc.vector.tensor_copy)
+        quantize(page_code[1], page_scale[1], woven[1], 0, BANK)
+        weave(1, cut, T2, nc.vector.tensor_copy)
+        for i in range(rows):
+            score_pass(1, i, 0)
+        quantize(page_code[1], page_scale[1], woven[1], BANK, T2)
+        for i in range(rows):
+            score_pass(1, i, 1)
+
+        e_sb = [ring.tile([P, T2], F32, name="e_sb", tag="mid", align_bytes=ALIGN) for i in range(rows)]
+        nc.scalar.copy(e_sb[0][:, :BANK], e_acc[0, 0][:])
+        nc.vector.tensor_copy(e_sb[0][:, BANK:], e_acc[0, 1][:])
+        for i in range(1, rows):
+            for u in range(2):
+                nc.scalar.copy(e_sb[i][:, BANK * u : BANK * (u + 1)], e_acc[i, u][:])
+        for i in range(rows):
+            res = held("res%d" % i, [P, PICK], F32)
+            pieces = ((0, PICK),) if i < rows - 1 else ((0, PICK // 2), (PICK // 2, PICK))
+            for lo, hi in pieces:
+                nc.vector.tensor_tensor(
+                    res[:, lo:hi], e_sb[i][:].indirect(idx4[:, lo // 16 : hi // 16]), prior[:, i, lo:hi], ADD
+                )
+                nc.sync.dma_start(out[P * i : P * (i + 1), lo:hi], res[:, lo:hi])

@@ -1,6 +1,7 @@
 from contextlib import ExitStack
 
 import concourse.mybir as mybir
+from concourse.masks import make_identity
 
 K, T, S, T2, T3, S2, PICK = 1024, 2048, 512, 1024, 2048, 512, 512
 FLOPS = 4 * 2 * K * K * S + 2 * K * S2 * T2
@@ -36,14 +37,13 @@ def tile_list_binning_order_scores_kernel(
     with ExitStack() as ctx:
         lists = ctx.enter_context(tc.tile_pool(name="lists", bufs=1))
         keep = ctx.enter_context(tc.tile_pool(name="keep", bufs=1))
-        ring = ctx.enter_context(tc.tile_pool(name="ring", bufs=4))
-        psum = ctx.enter_context(tc.psum_pool(name="psum", bufs=8))
+        psum = ctx.enter_context(tc.psum_pool(name="psum", bufs=1))
 
-        def held(name, shape, dtype):
-            return keep.tile(shape, dtype, name=name, align_bytes=ALIGN)
+        def held(name, shape, dtype, on=None):
+            return keep.tile(shape, dtype, name=name, tag=on or name, align_bytes=ALIGN)
 
-        def bank(name):
-            return psum.tile([P, BANK], F32, name=name, tag="bank")
+        def bank(name, number):
+            return psum.tile([P, BANK], F32, name=name, tag="bank%d" % number)
 
         idx = lists.tile([P, S // 16], U16, name="idx")
         idx2 = lists.tile([P, S2 // 16], U16, name="idx2")
@@ -58,16 +58,20 @@ def tile_list_binning_order_scores_kernel(
         nc.vector.memset(w4_scale_raw[:].rearrange("p a c -> p (a c)").bitcast(I32), 0)
         nc.vector.memset(tab2_scale[:].bitcast(I32), 0)
 
+        identity = held("identity", [P, P], F32)
+        make_identity(nc, identity[:])
+        wgs_raw = held("wgs_raw", [P, S], F32)
+        nc.sync.dma_start(wgs_raw[:], wgs)
         w4_raw = held("w4_raw", [P, PASSES, K // 2], I32)
         tab_word = [held("tab_word%d" % a, [P, T], I32) for a in range(PASSES)]
         nc.sync.dma_start(w4_raw[:], w4_words.bitcast(I32).rearrange("a p w -> p a w"))
         nc.sync.dma_start(idx[:], offs)
 
         def load_scales(plane, rows_in):
-            for quad in range(4):
+            for r in range(4):
                 nc.sync.dma_start(
-                    plane[32 * quad : 32 * quad + 4].bitcast(I32),
-                    rows_in[:, 4 * quad : 4 * quad + 4, :].bitcast(I32).rearrange("a r w -> r a w"),
+                    plane[r:P:32].bitcast(I32),
+                    rows_in.bitcast(I32).rearrange("a (q r) w -> r q a w", r=4)[r],
                 )
 
         load_scales(tab_scale, tab_scales)
@@ -78,47 +82,60 @@ def tile_list_binning_order_scores_kernel(
         w1_raw = {}
         for b in range(PASSES):
             for a in range(PASSES):
-                w1_raw[a, b] = ring.tile([P, PACK, PASS], F32, name="w1_raw", tag="wide", align_bytes=ALIGN)
+                w1_raw[a, b] = held("w1_raw%d%d" % (a, b), [P, PACK, PASS], F32)
                 nc.sync.dma_start(
                     w1_raw[a, b][:],
                     w1[PASS * a : PASS * (a + 1), PASS * b : PASS * (b + 1)].rearrange("(p i) c -> p i c", i=PACK),
                 )
+                if (a, b) == (0, 0):
+                    nc.sync.dma_start(idx2[:], offs2)
+                    nc.sync.dma_start(idx3[:], offs3)
 
-        nc.sync.dma_start(idx3[:], offs3)
-        gain = [held("gain%d" % u, [P, 2, S], F32) for u in range(2)]
         page = {(a, t): held("page%d%d" % (a, t), [P, T2], F32) for a in range(PASSES) for t in range(PACK)}
-        wgs_rows = wgs.rearrange("(m t) j -> m t j", t=PACK)
         page_rows = page0.rearrange("(a p t) c -> a t p c", a=PASSES, t=PACK)
+        tab2_word = [held("tab2_word%d" % a, [P, T3], I32) for a in range(PASSES)]
+        blend = held("blend", [P, S2 // P], F32)
+        prior = held("prior", [P, S2 // P, PICK], F32)
 
-        def load_gain(u):
-            for quad in range(4):
-                nc.sync.dma_start(gain[u][32 * quad : 32 * quad + 32], wgs_rows[:, 2 * u : 2 * u + 2, :])
+        def load_tab2(a):
+            nc.sync.dma_start(tab2_word[a][:], tab2_words[a].rearrange("p n i -> p (n i)").bitcast(I32))
 
-        for u in range(2):
-            load_gain(u)
-            for t in (2 * u, 2 * u + 1):
-                nc.sync.dma_start(page[0, t][:], page_rows[0, t])
-
-        nc.sync.dma_start(idx2[:], offs2)
-        for quad in range(4):
+        for quad in (0, 2, 1, 3):
             nc.sync.dma_start(
                 tab2_scale[32 * quad : 32 * quad + 8].bitcast(I32),
                 tab2_scales[:, 4 * quad : 4 * quad + 4, :].bitcast(I32),
             )
-        tab2_word = [held("tab2_word%d" % a, [P, T3], I32) for a in range(PASSES)]
-        for a in range(PASSES):
-            nc.sync.dma_start(tab2_word[a][:], tab2_words[a].rearrange("p n i -> p (n i)").bitcast(I32))
+        for t in (0, 1):
+            nc.sync.dma_start(page[0, t][:], page_rows[0, t])
+        load_tab2(0)
+        for t in (2, 3):
+            nc.sync.dma_start(page[0, t][:], page_rows[0, t])
         nc.sync.dma_start(idx4[:], offs4)
-        blend = held("blend", [P, S2 // P], F32)
         with nc.allow_non_contiguous_dma(reason="one weight to a partition"):
             nc.sync.dma_start(blend[:], be.rearrange("(i p) -> p i", p=P))
-        prior = held("prior", [P, S2 // P, PICK], F32)
         nc.sync.dma_start(prior[:], ref.rearrange("(i p) m -> p i m", p=P))
-        for t in range(PACK):
+        load_tab2(1)
+        last_order = (2, 0, 1, 3)
+        for t in last_order:
             nc.sync.dma_start(page[1, t][:], page_rows[1, t])
 
+        turned = bank("turned", 4)
+        for g in range(S // P):
+            nc.tensor.transpose(turned[:, P * g : P * (g + 1)], wgs_raw[:, P * g : P * (g + 1)], identity[:])
+        spread = held("spread", [P, S // P, PACK, 4, 32], F32)
+        for quad in range(4):
+            nc.scalar.copy(spread[:, :, :, quad, :], turned[:].rearrange("p (g m t) -> p g t m", g=S // P, t=PACK))
+        gain = [held("gain%d" % t, [P, S], F32) for t in range(PACK)]
+        for t in range(PACK):
+            back = bank("back", t)
+            for g in range(S // P):
+                nc.tensor.transpose(
+                    back[:, P * g : P * (g + 1)], spread[:, g, t].rearrange("p q m -> p (q m)"), identity[:]
+                )
+            nc.scalar.copy(gain[t][:], back[:])
+
         w4_code = [held("w4_code%d" % a, [P, 2 * K], U8) for a in range(PASSES)]
-        w4_scale = [held("w4_scale%d" % a, [P, K], U8) for a in range(PASSES)]
+        w4_scale = [held("w4_scale0", [P, K], U8, "spread"), held("w4_scale1", [P, K], U8)]
         v_code = [held("v_code%d" % a, [P, S], I32) for a in range(PASSES)]
         v_scale = [held("v_scale%d" % a, [P, S], U8) for a in range(PASSES)]
 
@@ -174,7 +191,7 @@ def tile_list_binning_order_scores_kernel(
             nc.vector.quantize_mx(code[:, lo:hi].bitcast(FP8X4), scale[:, lo:hi], src[:, PACK * lo : PACK * hi])
 
         def prepare_w1(a, b, split):
-            rounded = ring.tile([P, PACK * PASS], BF16, name="w1_bf", tag="mid", align_bytes=ALIGN)
+            rounded = held("w1_bf%d%d" % (a, b), [P, PACK * PASS], BF16)
             dst = rounded[:].rearrange("p (t m i) -> p m t i", t=PACK, i=PACK)
             src = w1_raw[a, b][:].rearrange("p i (m t) -> p m t i", t=PACK)
             nc.vector.tensor_scalar(dst[:, :split], src[:, :split], -1.0, None, MULT)
@@ -184,170 +201,214 @@ def tile_list_binning_order_scores_kernel(
             w1_scale[a, b] = held("w1_scale%d%d" % (a, b), [P, PASS], U8)
             quantize(w1_code[a, b], w1_scale[a, b], rounded, 0, PASS)
 
-        chunks = S // CHUNK
-        q_bf = [held("q_bf%d" % b, [P, PACK * S], BF16) for b in range(PASSES)]
-        p_bf = [held("p_bf%d" % b, [P, PACK * S], BF16) for b in range(PASSES)]
-        q_code = [held("q_code%d" % b, [P, S], I32) for b in range(PASSES)]
-        p_code = [held("p_code%d" % b, [P, S], I32) for b in range(PASSES)]
-        q_scale = [held("q_scale%d" % b, [P, S], U8) for b in range(PASSES)]
-        p_scale = [held("p_scale%d" % b, [P, S], U8) for b in range(PASSES)]
-
-        q_acc = {(b, c): bank("q_acc") for b in range(PASSES) for c in range(chunks)}
-        for a in range(PASSES):
-            for b in range(PASSES):
-                for c in range(chunks):
-                    first_stage_pass(q_acc[b, c], w4_side, a, b, c)
-        prepare_w1(0, 0, 96)
-        for c in range(chunks):
-            rectify(q_bf[0], q_acc[0, c], c, 1.0, False)
-        prepare_w1(1, 0, P)
-        for c in range(chunks):
-            rectify(q_bf[1], q_acc[1, c], c, 1.0, False)
-        quantize(q_code[0], q_scale[0], q_bf[0], 0, S)
-
-        p_acc = {(b, c): bank("p_acc") for b in range(PASSES) for c in range(chunks)}
-        for a in range(PASSES):
-            for c in range(chunks):
-                first_stage_pass(p_acc[0, c], w1_side, a, 0, c)
-        prepare_w1(0, 1, P)
-        quantize(q_code[1], q_scale[1], q_bf[1], 0, S)
-        for c in range(chunks):
-            rectify(p_bf[0], p_acc[0, c], c, -1.0, False)
-        for c in range(chunks):
-            first_stage_pass(p_acc[1, c], w1_side, 0, 1, c)
-        prepare_w1(1, 1, 88)
-        quantize(p_code[0], p_scale[0], p_bf[0], 0, S)
-
         half = S // 2
-        head_acc = [bank("head_acc") for u in range(2)]
+        rounded_act, act_code, act_scale, first_acc = {}, {}, {}, {}
 
-        def head_q(u):
-            cols = slice(half * u, half * (u + 1))
+        def rectify_half(name, b, u, vector_chunks=()):
+            for c in range(2):
+                rectify(rounded_act[name, b, u], first_acc[name, b, 2 * u + c], c,
+                        1.0 if name == "q" else -1.0, c in vector_chunks)
+
+        def quantize_p(b, u, on=None):
+            act_code["p", b, u] = held("p_code%d%d" % (b, u), [P, half], I32)
+            act_scale["p", b, u] = held("p_scale%d%d" % (b, u), [P, half], U8, on)
+            quantize(act_code["p", b, u], act_scale["p", b, u], rounded_act["p", b, u], 0, half)
+
+        def quantize_q(u, on):
+            code = held("q_code%d" % u, [P, S], I32)
+            scale = held("q_scale%d" % u, [P, S], U8, on)
+            quantize(code, scale, q_bf[:, u, :], 0, S)
+            for b in range(PASSES):
+                act_code["q", b, u] = code[:, half * b : half * (b + 1)]
+                act_scale["q", b, u] = scale[:, half * b : half * (b + 1)]
+
+        def open_p(b, u):
+            rounded_act["p", b, u] = held("p_bf%d%d" % (b, u), [P, PACK * half], BF16)
+
+        def first_stage(name, a, b, u):
+            for c in (2 * u, 2 * u + 1):
+                first_stage_pass(first_acc[name, b, c], w4_side if name == "q" else w1_side, a, b, c)
+
+        def open_first(name, b, u, number):
+            for c in range(2):
+                first_acc[name, b, 2 * u + c] = bank(name + "_acc", number + c)
+
+        def second_q(acc, b, t, u, start):
             for a in range(PASSES):
-                for t in range(2):
-                    mx(head_acc[u][:, half * t : half * (t + 1)], w1_side(a, 0, t), q_code[a], q_scale[a], cols,
-                       a == 0 and t == 0, False)
+                mx(acc, w1_side(a, b, t), act_code["q", a, u], act_scale["q", a, u], slice(0, half),
+                   start and a == 0, False)
 
-        def head_p(u, a):
-            for t in range(2):
-                for c in range(2):
-                    lo = half * u + CHUNK * c
-                    at = half * t + CHUNK * c
-                    mx(head_acc[u][:, at : at + CHUNK], w4_side(a, 0, t), p_code[a], p_scale[a],
-                       slice(lo, lo + CHUNK), False, a == PASSES - 1 and t == 1 and c == 1)
+        def second_p(acc, a, b, t, u, stop):
+            for c in range(2):
+                cols = slice(CHUNK * c, CHUNK * (c + 1))
+                mx(acc[:, cols], w4_side(a, b, t), act_code["p", a, u], act_scale["p", a, u], cols,
+                   False, stop and c == 1)
 
-        for c in range(2):
-            first_stage_pass(p_acc[1, c], w1_side, 1, 1, c)
-        head_q(0)
-        head_p(0, 0)
-        for c in range(2, chunks):
-            first_stage_pass(p_acc[1, c], w1_side, 1, 1, c)
+        for u in range(2):
+            for b in range(PASSES):
+                open_first("q", b, u, 4 * u + 2 * b)
+        for a in range(PASSES):
+            for u in range(2):
+                for b in range(PASSES):
+                    first_stage("q", a, b, u)
+        prepare_w1(0, 0, 96)
+        q_bf = held("q_bf", [P, 2, PASSES * PACK * half], BF16, "w1_raw00")
+        for u in range(2):
+            for b in range(PASSES):
+                rounded_act["q", b, u] = q_bf[:, u, PACK * half * b : PACK * half * (b + 1)]
+        for b in range(PASSES):
+            rectify_half("q", b, 0)
+        prepare_w1(1, 0, P)
+        quantize_q(0, "w1_raw10")
+        for b in range(PASSES):
+            rectify_half("q", b, 1)
 
-        rectify(p_bf[1], p_acc[1, 0], 0, -1.0, False)
-        rectify(p_bf[1], p_acc[1, 1], 1, -1.0, True)
-        quantize(p_code[1], p_scale[1], p_bf[1], 0, half)
-        rectify(p_bf[1], p_acc[1, 2], 2, -1.0, False)
-        head_p(0, 1)
-        head_sb = [held("head_sb%d" % u, [P, 2, half], F32) for u in range(2)]
-        nc.scalar.copy(head_sb[0][:].rearrange("p t j -> p (t j)"), head_acc[0][:])
-        rectify(p_bf[1], p_acc[1, 3], 3, -1.0, False)
+        open_first("p", 0, 0, 0)
+        for a in range(PASSES):
+            first_stage("p", a, 0, 0)
+        prepare_w1(0, 1, P)
+        open_p(0, 0)
+        rectify_half("p", 0, 0)
+        head_acc = {(0, g): bank("head_acc", 4 + g) for g in range(2)}
+        for t in range(PACK):
+            second_q(head_acc[0, t // 2][:, half * (t % 2) : half * (t % 2 + 1)], 0, t, 0, t % 2 == 0)
+        open_first("p", 1, 0, 2)
+        first_stage("p", 0, 1, 0)
+        prepare_w1(1, 1, 88)
+        first_stage("p", 1, 1, 0)
+        quantize_p(0, 0, "w1_raw11")
+        quantize_q(1, "p_bf00")
+        open_p(1, 0)
+        rectify_half("p", 1, 0, (1,))
+        quantize_p(1, 0)
+        v2_scale = held("v2_scale", [P, S2], U8, "p_bf10")
+        nc.vector.tensor_copy(v2_scale[:], tab2_scale[:].indirect(idx2[:]))
+
+        head_sb = {}
+
+        def finish_head(u):
+            for a in range(PASSES):
+                for t in range(PACK):
+                    second_p(head_acc[u, t // 2][:, half * (t % 2) : half * (t % 2 + 1)], a, 0, t, u,
+                             a == PASSES - 1 and t % 2 == 1)
+
+        def empty_head(u, g, on=None):
+            head_sb[u, g] = held("head_sb%d%d" % (u, g), [P, 2, half], F32, on)
+            nc.scalar.copy(head_sb[u, g][:].rearrange("p t j -> p (t j)"), head_acc[u, g][:])
 
         def scatter(a, t, src, lo, hi):
             nc.vector.tensor_tensor(
-                page[a, t][:].indirect(idx3[:, lo // 16 : hi // 16]), src, gain[t // 2][:, t % 2, lo:hi], MULT
+                page[a, t][:].indirect(idx3[:, lo // 16 : hi // 16]), src, gain[t][:, lo:hi], MULT
             )
 
-        scatter(0, 0, head_sb[0][:, 0, :], 0, half)
-        quantize(p_code[1], p_scale[1], p_bf[1], half, S)
-        scatter(0, 1, head_sb[0][:, 1, :], 0, half)
-        head_q(1)
-        head_p(1, 0)
-        head_p(1, 1)
-        nc.scalar.copy(head_sb[1][:].rearrange("p t j -> p (t j)"), head_acc[1][:])
+        finish_head(0)
+        empty_head(0, 0)
 
-        h_sb = {}
-        whole = slice(0, S)
-        rest = [(0, 2), (0, 3)] + [(1, t) for t in range(PACK)]
-        for b, t in rest:
-            acc = bank("h_acc")
+        open_first("p", 1, 1, 6)
+        open_first("p", 0, 1, 2)
+        for b in (1, 0):
             for a in range(PASSES):
-                mx(acc[:], w1_side(a, b, t), q_code[a], q_scale[a], whole, a == 0, False)
-            for a in range(PASSES):
-                mx(acc[:], w4_side(a, b, t), p_code[a], p_scale[a], whole, False, a == PASSES - 1)
-            h_sb[b, t] = keep.tile([P, S], F32, name="h_sb", tag="h_sb%d%d" % (b, t), align_bytes=ALIGN)
-            nc.scalar.copy(h_sb[b, t][:], acc[:])
-
-        planes = [ring.tile([P, PACK, T2], BF16, name="planes", tag="wide", align_bytes=ALIGN) for a in range(PASSES)]
-        woven = [ring.tile([P, PACK * T2], BF16, name="woven", tag="wide", align_bytes=ALIGN) for a in range(PASSES)]
-        page_code = [held("page_code%d" % a, [P, T2], I32) for a in range(PASSES)]
-        page_scale = [None, held("page_scale1", [P, T2], U8)]
-
-        def round_plane(a, t, lo, hi, copy):
-            copy(planes[a][:, t, lo:hi], page[a, t][:, lo:hi])
-
-        def weave(a, lo, hi, copy):
-            copy(
-                woven[a][:, PACK * lo : PACK * hi].rearrange("p (c i t) -> p c t i", i=4, t=PACK),
-                planes[a][:, :, lo:hi].rearrange("p t (c i) -> p c t i", i=4),
-            )
-
+                first_stage("p", a, b, 1)
+            open_p(b, 1)
+            rectify_half("p", b, 1)
         for t in range(2):
-            scatter(0, t, head_sb[1][:, t, :], half, S)
-            round_plane(0, t, 0, T2, nc.scalar.copy)
-        for t in range(2, PACK):
-            scatter(0, t, h_sb[0, t][:], 0, S)
-            round_plane(0, t, 0, T2, nc.scalar.copy)
-        for u in range(2):
-            weave(0, BANK * u, BANK * (u + 1), nc.scalar.copy)
+            scatter(0, t, head_sb[0, 0][:, t, :], 0, half)
+        for b in (1, 0):
+            quantize_p(b, 1)
+        empty_head(0, 1, "p_bf11")
+        v2_code = [held("v2_code0", [P, S2], I32, "p_bf01"), None]
 
-        v2_code = [held("v2_code%d" % a, [P, S2], I32) for a in range(PASSES)]
-        v2_scale = held("v2_scale", [P, S2], U8)
-        nc.vector.tensor_copy(v2_scale[:], tab2_scale[:].indirect(idx2[:]))
-        for a in range(PASSES):
+        def gather_tab2(a):
             nc.vector.tensor_copy(v2_code[a][:].bitcast(U32), tab2_word[a][:].bitcast(U32).indirect(idx2[:]))
 
+        gather_tab2(0)
+        for t in range(2, PACK):
+            scatter(0, t, head_sb[0, 1][:, t % 2, :], 0, half)
+        for g in range(2):
+            head_acc[1, g] = bank("head_acc", g)
+        for t in range(PACK):
+            second_q(head_acc[1, t // 2][:, half * (t % 2) : half * (t % 2 + 1)], 0, t, 1, t % 2 == 0)
+        finish_head(1)
+        for g in range(2):
+            empty_head(1, g)
+
+        h_acc, h_sb = {}, {}
+
+        def empty_h(t, on=None):
+            h_sb[t] = held("h_sb%d" % t, [P, S], F32, on)
+            nc.scalar.copy(h_sb[t][:], h_acc[t][:])
+
+        for n, t in enumerate(last_order):
+            h_acc[t] = bank("h_acc", 4 + n)
+            for u in range(2):
+                second_q(h_acc[t][:, half * u : half * (u + 1)], 1, t, u, u == 0)
+            for u in range(2):
+                for a in range(PASSES):
+                    second_p(h_acc[t][:, half * u : half * (u + 1)], a, 1, t, u, u == 1 and a == PASSES - 1)
+            if t != 3:
+                empty_h(t)
+
+        pairs = {(a, u): held("pairs%d%d" % (a, u), [P, 2, BANK, 2], BF16, "w1_bf%d%d" % (a, u))
+                 for a in range(PASSES) for u in range(2)}
+        woven = [held("woven0", [P, PACK * T2], BF16, "w1_raw01"), held("woven1", [P, PACK * T2], BF16, "w1_raw10")]
+        page_code = [held("page_code%d" % a, [P, T2], I32) for a in range(PASSES)]
+        page_scale = [None, held("page_scale1", [P, T2], U8)]
         rows = S2 // P
+
+        for i in range(rows):
+            nc.scalar.activation(prior[:, i, :], prior[:, i, :], COPY, scale=blend[:, i : i + 1])
+
+        def round_in(a, t, u, copy):
+            copy(pairs[a, u][:, t // 2, :, t % 2], page[a, t][:, BANK * u : BANK * (u + 1)])
+
+        def weave(a, u, copy):
+            words = pairs[a, u][:].rearrange("p g c e -> p g (c e)").bitcast(F32)
+            dst = woven[a][:, PACK * BANK * u : PACK * BANK * (u + 1)].bitcast(F32)
+            copy(dst.rearrange("p (c g) -> p c g", g=2), words.rearrange("p g c -> p c g"))
+
+        for t in range(PACK):
+            scatter(0, t, head_sb[1, t // 2][:, t % 2, :], half, S)
+            for u in range(2):
+                round_in(0, t, u, nc.scalar.copy)
+        for u in range(2):
+            weave(0, u, nc.scalar.copy)
+
+        v2_code[1] = held("v2_code1", [P, S2], I32, "head_sb11")
+        gather_tab2(1)
+
         e_acc = {}
 
         def score_pass(a, i, u):
             side = (v2_code[a][:, P * i : P * (i + 1)].bitcast(FP8X4), v2_scale[4 * a :, P * i : P * (i + 1)])
             mx(e_acc[i, u][:], side, page_code[a], page_scale[a], slice(BANK * u, BANK * (u + 1)), a == 0, a == 1)
 
-        scatter(1, 0, h_sb[1, 0][:], 0, S)
-        round_plane(1, 0, 0, T2, nc.scalar.copy)
-        scatter(1, 1, h_sb[1, 1][:], 0, S)
-        round_plane(1, 1, 0, T2, nc.scalar.copy)
-        for i in range(rows):
-            nc.scalar.activation(prior[:, i, :], prior[:, i, :], COPY, scale=blend[:, i : i + 1])
-        scatter(1, 2, h_sb[1, 2][:], 0, S)
-        round_plane(1, 2, 0, T2, nc.scalar.copy)
-        page_scale[0] = keep.tile([P, T2], U8, name="page_scale0", tag="h_sb12", align_bytes=ALIGN)
+        for t in last_order[:3]:
+            scatter(1, t, h_sb[t][:], 0, S)
+            for u in range(2):
+                round_in(1, t, u, nc.scalar.copy)
+            if t == 2:
+                empty_h(3, "page12")
+        page_scale[0] = held("page_scale0", [P, T2], U8, "h_sb1")
         quantize(page_code[0], page_scale[0], woven[0], 0, T2)
         for u in range(2):
             for i in range(rows):
-                e_acc[i, u] = bank("e_acc")
+                e_acc[i, u] = bank("e_acc", 4 * u + i)
                 score_pass(0, i, u)
-        scatter(1, 3, h_sb[1, 3][:], 0, S)
+        scatter(1, 3, h_sb[3][:], 0, S)
 
-        cut = 896
-        round_plane(1, 3, 0, BANK, nc.vector.tensor_copy)
-        round_plane(1, 3, BANK, T2, nc.scalar.copy)
-        weave(1, BANK, cut, nc.scalar.copy)
-        weave(1, 0, BANK, nc.vector.tensor_copy)
-        quantize(page_code[1], page_scale[1], woven[1], 0, BANK)
-        weave(1, cut, T2, nc.vector.tensor_copy)
-        for i in range(rows):
-            score_pass(1, i, 0)
-        quantize(page_code[1], page_scale[1], woven[1], BANK, T2)
-        for i in range(rows):
-            score_pass(1, i, 1)
+        for u, copy in ((0, nc.vector.tensor_copy), (1, nc.scalar.copy)):
+            round_in(1, 3, u, copy)
+            weave(1, u, copy)
+        for u in range(2):
+            quantize(page_code[1], page_scale[1], woven[1], BANK * u, BANK * (u + 1))
+            for i in range(rows):
+                score_pass(1, i, u)
 
-        e_sb = [ring.tile([P, T2], F32, name="e_sb", tag="mid", align_bytes=ALIGN) for i in range(rows)]
-        nc.scalar.copy(e_sb[0][:, :BANK], e_acc[0, 0][:])
-        nc.vector.tensor_copy(e_sb[0][:, BANK:], e_acc[0, 1][:])
-        for i in range(1, rows):
+        e_sb = [held("e_sb%d" % i, [P, T2], F32, "page0%d" % i) for i in range(rows)]
+        for i in range(rows):
             for u in range(2):
-                nc.scalar.copy(e_sb[i][:, BANK * u : BANK * (u + 1)], e_acc[i, u][:])
+                copy = nc.vector.tensor_copy if (i, u) == (1, 0) else nc.scalar.copy
+                copy(e_sb[i][:, BANK * u : BANK * (u + 1)], e_acc[i, u][:])
         for i in range(rows):
             res = held("res%d" % i, [P, PICK], F32)
             pieces = ((0, PICK),) if i < rows - 1 else ((0, PICK // 2), (PICK // 2, PICK))

@@ -24,9 +24,18 @@ P = 128
 PACK = 4
 PASS = P * PACK
 PASSES = K // PASS
+QUADS = 4
+QUAD = P // QUADS
+SCALE_ROWS = 4
+LANES = 16
 BANK = 512
 CHUNK = 128
+HALF = S // 2
+QUARTER = T2 // 4
+OUT_TILES = S2 // P
 ALIGN = 64
+FIRST_SHARE, LAST_SHARE = 96, 88
+LAST_ORDER = (2, 0, 1, 3)
 
 
 def tile_list_binning_order_scores_kernel(
@@ -45,10 +54,10 @@ def tile_list_binning_order_scores_kernel(
         def bank(name, number):
             return psum.tile([P, BANK], F32, name=name, tag="bank%d" % number)
 
-        idx = lists.tile([P, S // 16], U16, name="idx")
-        idx2 = lists.tile([P, S2 // 16], U16, name="idx2")
-        idx3 = lists.tile([P, S // 16], U16, name="idx3")
-        idx4 = lists.tile([P, PICK // 16], U16, name="idx4")
+        idx = lists.tile([P, S // LANES], U16, name="idx")
+        idx2 = lists.tile([P, S2 // LANES], U16, name="idx2")
+        idx3 = lists.tile([P, S // LANES], U16, name="idx3")
+        idx4 = lists.tile([P, PICK // LANES], U16, name="idx4")
 
         w4_scale_raw = held("w4_scale_raw", [P, PASSES, K], U8)
         tab_scale = held("tab_scale", [P, PASSES, T], U8)
@@ -67,11 +76,11 @@ def tile_list_binning_order_scores_kernel(
         nc.sync.dma_start(w4_raw[:], w4_words.bitcast(I32).rearrange("a p w -> p a w"))
         nc.sync.dma_start(idx[:], offs)
 
-        def load_scales(plane, rows_in):
-            for r in range(4):
+        def load_scales(tile, scale_rows):
+            for r in range(SCALE_ROWS):
                 nc.sync.dma_start(
-                    plane[r:P:32].bitcast(I32),
-                    rows_in.bitcast(I32).rearrange("a (q r) w -> r q a w", r=4)[r],
+                    tile[r:P:QUAD].bitcast(I32),
+                    scale_rows.bitcast(I32).rearrange("a (q r) w -> r q a w", r=SCALE_ROWS)[r],
                 )
 
         load_scales(tab_scale, tab_scales)
@@ -94,16 +103,16 @@ def tile_list_binning_order_scores_kernel(
         page = {(a, t): held("page%d%d" % (a, t), [P, T2], F32) for a in range(PASSES) for t in range(PACK)}
         page_rows = page0.rearrange("(a p t) c -> a t p c", a=PASSES, t=PACK)
         tab2_word = [held("tab2_word%d" % a, [P, T3], I32) for a in range(PASSES)]
-        blend = held("blend", [P, S2 // P], F32)
-        prior = held("prior", [P, S2 // P, PICK], F32)
+        blend = held("blend", [P, OUT_TILES], F32)
+        prior = held("prior", [P, OUT_TILES, PICK], F32)
 
         def load_tab2(a):
             nc.sync.dma_start(tab2_word[a][:], tab2_words[a].rearrange("p n i -> p (n i)").bitcast(I32))
 
         for quad in (0, 2, 1, 3):
             nc.sync.dma_start(
-                tab2_scale[32 * quad : 32 * quad + 8].bitcast(I32),
-                tab2_scales[:, 4 * quad : 4 * quad + 4, :].bitcast(I32),
+                tab2_scale[QUAD * quad : QUAD * quad + PASSES * SCALE_ROWS].bitcast(I32),
+                tab2_scales[:, SCALE_ROWS * quad : SCALE_ROWS * (quad + 1), :].bitcast(I32),
             )
         for t in (0, 1):
             nc.sync.dma_start(page[0, t][:], page_rows[0, t])
@@ -115,22 +124,23 @@ def tile_list_binning_order_scores_kernel(
             nc.sync.dma_start(blend[:], be.rearrange("(i p) -> p i", p=P))
         nc.sync.dma_start(prior[:], ref.rearrange("(i p) m -> p i m", p=P))
         load_tab2(1)
-        last_order = (2, 0, 1, 3)
-        for t in last_order:
+        for t in LAST_ORDER:
             nc.sync.dma_start(page[1, t][:], page_rows[1, t])
 
         turned = bank("turned", 4)
-        for g in range(S // P):
-            nc.tensor.transpose(turned[:, P * g : P * (g + 1)], wgs_raw[:, P * g : P * (g + 1)], identity[:])
-        spread = held("spread", [P, S // P, PACK, 4, 32], F32)
-        for quad in range(4):
-            nc.scalar.copy(spread[:, :, :, quad, :], turned[:].rearrange("p (g m t) -> p g t m", g=S // P, t=PACK))
+        for blk in range(S // P):
+            nc.tensor.transpose(turned[:, P * blk : P * (blk + 1)], wgs_raw[:, P * blk : P * (blk + 1)], identity[:])
+        spread = held("spread", [P, S // P, PACK, QUADS, QUAD], F32)
+        for quad in range(QUADS):
+            nc.scalar.copy(
+                spread[:, :, :, quad, :], turned[:].rearrange("p (blk m t) -> p blk t m", blk=S // P, t=PACK)
+            )
         gain = [held("gain%d" % t, [P, S], F32) for t in range(PACK)]
         for t in range(PACK):
             back = bank("back", t)
-            for g in range(S // P):
+            for blk in range(S // P):
                 nc.tensor.transpose(
-                    back[:, P * g : P * (g + 1)], spread[:, g, t].rearrange("p q m -> p (q m)"), identity[:]
+                    back[:, P * blk : P * (blk + 1)], spread[:, blk, t].rearrange("p q m -> p (q m)"), identity[:]
                 )
             nc.scalar.copy(gain[t][:], back[:])
 
@@ -139,109 +149,98 @@ def tile_list_binning_order_scores_kernel(
         v_code = [held("v_code%d" % a, [P, S], I32) for a in range(PASSES)]
         v_scale = [held("v_scale%d" % a, [P, S], U8) for a in range(PASSES)]
 
-        def order_words(a):
+        def sort_columns(dst, src):
             nc.vector.tensor_copy(
-                w4_code[a][:].bitcast(U16).rearrange("p (b t m) -> p b t m", b=PASSES, t=PACK),
-                w4_raw[:, a, :].bitcast(U16).rearrange("p (b m t) -> p b t m", b=PASSES, t=PACK),
-            )
-
-        def order_scales(a):
-            nc.vector.tensor_copy(
-                w4_scale[a][:].rearrange("p (b t m) -> p b t m", b=PASSES, t=PACK),
-                w4_scale_raw[:, a, :].rearrange("p (b m t) -> p b t m", b=PASSES, t=PACK),
+                dst.rearrange("p (b t m) -> p b t m", b=PASSES, t=PACK),
+                src.rearrange("p (b m t) -> p b t m", b=PASSES, t=PACK),
             )
 
         for a in range(PASSES):
-            order_words(a)
+            sort_columns(w4_code[a][:].bitcast(U16), w4_raw[:, a, :].bitcast(U16))
             nc.vector.tensor_copy(v_code[a][:].bitcast(U32), tab_word[a][:].bitcast(U32).indirect(idx[:]))
-            order_scales(a)
+            sort_columns(w4_scale[a][:], w4_scale_raw[:, a, :])
             nc.vector.tensor_copy(v_scale[a][:], tab_scale[:, a, :].indirect(idx[:]))
 
         w1_code, w1_scale = {}, {}
 
-        def w4_side(a, b, t):
-            c = PASS * b + P * t
-            return w4_code[a][:, 2 * c : 2 * (c + P)].bitcast(FP4X4), w4_scale[a][:, c : c + P]
+        def w4_columns(a, b, t):
+            col = PASS * b + P * t
+            return w4_code[a][:, 2 * col : 2 * (col + P)].bitcast(FP4X4), w4_scale[a][:, col : col + P]
 
-        def w1_side(a, b, t):
-            c = P * t
-            return w1_code[a, b][:, c : c + P].bitcast(FP8X4), w1_scale[a, b][:, c : c + P]
+        def w1_columns(a, b, t):
+            col = P * t
+            return w1_code[a, b][:, col : col + P].bitcast(FP8X4), w1_scale[a, b][:, col : col + P]
 
-        def mx(acc, side, code, scale, cols, start, stop):
+        def mx(acc, stationary, code, scale, cols, start, stop):
             nc.tensor.matmul_mx(
-                out=acc, lhsT=side[0], lhsT_scale=side[1],
+                out=acc, lhsT=stationary[0], lhsT_scale=stationary[1],
                 rhs=code[:, cols].bitcast(FP8X4), rhs_scale=scale[:, cols], start=start, stop=stop,
             )
-
-        def first_stage_pass(acc, side_of, a, b, c):
-            cols = slice(CHUNK * c, CHUNK * (c + 1))
-            for t in range(PACK):
-                mx(acc[:, CHUNK * t : CHUNK * (t + 1)], side_of(a, b, t), v_code[a], v_scale[a], cols,
-                   a == 0 and t == 0, a == PASSES - 1 and t == PACK - 1)
-
-        def rectify(dst, acc, c, sign, on_vector):
-            woven = dst[:, PACK * CHUNK * c : PACK * CHUNK * (c + 1)].rearrange("p (n t) -> p n t", t=PACK)
-            src = acc[:].rearrange("p (t n) -> p n t", t=PACK)
-            if on_vector:
-                nc.vector.tensor_scalar(woven, src, sign, 0.0, MULT, MAX)
-            else:
-                nc.scalar.activation(woven, src, RELU, scale=sign)
 
         def quantize(code, scale, src, lo, hi):
             nc.vector.quantize_mx(code[:, lo:hi].bitcast(FP8X4), scale[:, lo:hi], src[:, PACK * lo : PACK * hi])
 
-        def prepare_w1(a, b, split):
+        def prepare_w1(a, b, share):
             rounded = held("w1_bf%d%d" % (a, b), [P, PACK * PASS], BF16)
             dst = rounded[:].rearrange("p (t m i) -> p m t i", t=PACK, i=PACK)
             src = w1_raw[a, b][:].rearrange("p i (m t) -> p m t i", t=PACK)
-            nc.vector.tensor_scalar(dst[:, :split], src[:, :split], -1.0, None, MULT)
-            if split < P:
-                nc.scalar.activation(dst[:, split:], src[:, split:], COPY, scale=-1.0)
+            nc.vector.tensor_scalar(dst[:, :share], src[:, :share], -1.0, None, MULT)
+            if share < P:
+                nc.scalar.activation(dst[:, share:], src[:, share:], COPY, scale=-1.0)
             w1_code[a, b] = held("w1_code%d%d" % (a, b), [P, PASS], I32)
             w1_scale[a, b] = held("w1_scale%d%d" % (a, b), [P, PASS], U8)
             quantize(w1_code[a, b], w1_scale[a, b], rounded, 0, PASS)
 
-        half = S // 2
-        rounded_act, act_code, act_scale, first_acc = {}, {}, {}, {}
-
-        def rectify_half(name, b, u, vector_chunks=()):
-            for c in range(2):
-                rectify(rounded_act[name, b, u], first_acc[name, b, 2 * u + c], c,
-                        1.0 if name == "q" else -1.0, c in vector_chunks)
-
-        def quantize_p(b, u, on=None):
-            act_code["p", b, u] = held("p_code%d%d" % (b, u), [P, half], I32)
-            act_scale["p", b, u] = held("p_scale%d%d" % (b, u), [P, half], U8, on)
-            quantize(act_code["p", b, u], act_scale["p", b, u], rounded_act["p", b, u], 0, half)
-
-        def quantize_q(u, on):
-            code = held("q_code%d" % u, [P, S], I32)
-            scale = held("q_scale%d" % u, [P, S], U8, on)
-            quantize(code, scale, q_bf[:, u, :], 0, S)
-            for b in range(PASSES):
-                act_code["q", b, u] = code[:, half * b : half * (b + 1)]
-                act_scale["q", b, u] = scale[:, half * b : half * (b + 1)]
-
-        def open_p(b, u):
-            rounded_act["p", b, u] = held("p_bf%d%d" % (b, u), [P, PACK * half], BF16)
-
-        def first_stage(name, a, b, u):
-            for c in (2 * u, 2 * u + 1):
-                first_stage_pass(first_acc[name, b, c], w4_side if name == "q" else w1_side, a, b, c)
+        act_bf, act_code, act_scale, first_acc = {}, {}, {}, {}
 
         def open_first(name, b, u, number):
             for c in range(2):
                 first_acc[name, b, 2 * u + c] = bank(name + "_acc", number + c)
 
+        def first_stage(name, a, b, u):
+            columns = w4_columns if name == "q" else w1_columns
+            for chunk in (2 * u, 2 * u + 1):
+                for t in range(PACK):
+                    mx(first_acc[name, b, chunk][:, CHUNK * t : CHUNK * (t + 1)], columns(a, b, t),
+                       v_code[a], v_scale[a], slice(CHUNK * chunk, CHUNK * (chunk + 1)),
+                       a == 0 and t == 0, a == PASSES - 1 and t == PACK - 1)
+
+        def rectify(name, b, u, vector_chunks=()):
+            sign = 1.0 if name == "q" else -1.0
+            for c in range(2):
+                dst = act_bf[name, b, u][:, PACK * CHUNK * c : PACK * CHUNK * (c + 1)]
+                dst = dst.rearrange("p (n t) -> p n t", t=PACK)
+                src = first_acc[name, b, 2 * u + c][:].rearrange("p (t n) -> p n t", t=PACK)
+                if c in vector_chunks:
+                    nc.vector.tensor_scalar(dst, src, sign, 0.0, MULT, MAX)
+                else:
+                    nc.scalar.activation(dst, src, RELU, scale=sign)
+
+        def open_p(b, u):
+            act_bf["p", b, u] = held("p_bf%d%d" % (b, u), [P, PACK * HALF], BF16)
+
+        def quantize_p(b, u, on=None):
+            act_code["p", b, u] = held("p_code%d%d" % (b, u), [P, HALF], I32)
+            act_scale["p", b, u] = held("p_scale%d%d" % (b, u), [P, HALF], U8, on)
+            quantize(act_code["p", b, u], act_scale["p", b, u], act_bf["p", b, u], 0, HALF)
+
+        def quantize_q(u, on):
+            code = held("q_code%d" % u, [P, PASSES * HALF], I32)
+            scale = held("q_scale%d" % u, [P, PASSES * HALF], U8, on)
+            quantize(code, scale, q_bf[:, u, :], 0, PASSES * HALF)
+            for b in range(PASSES):
+                act_code["q", b, u] = code[:, HALF * b : HALF * (b + 1)]
+                act_scale["q", b, u] = scale[:, HALF * b : HALF * (b + 1)]
+
         def second_q(acc, b, t, u, start):
             for a in range(PASSES):
-                mx(acc, w1_side(a, b, t), act_code["q", a, u], act_scale["q", a, u], slice(0, half),
+                mx(acc, w1_columns(a, b, t), act_code["q", a, u], act_scale["q", a, u], slice(0, HALF),
                    start and a == 0, False)
 
         def second_p(acc, a, b, t, u, stop):
             for c in range(2):
                 cols = slice(CHUNK * c, CHUNK * (c + 1))
-                mx(acc[:, cols], w4_side(a, b, t), act_code["p", a, u], act_scale["p", a, u], cols,
+                mx(acc[:, cols], w4_columns(a, b, t), act_code["p", a, u], act_scale["p", a, u], cols,
                    False, stop and c == 1)
 
         for u in range(2):
@@ -251,56 +250,61 @@ def tile_list_binning_order_scores_kernel(
             for u in range(2):
                 for b in range(PASSES):
                     first_stage("q", a, b, u)
-        prepare_w1(0, 0, 96)
-        q_bf = held("q_bf", [P, 2, PASSES * PACK * half], BF16, "w1_raw00")
+        prepare_w1(0, 0, FIRST_SHARE)
+        q_bf = held("q_bf", [P, 2, PASSES * PACK * HALF], BF16, "w1_raw00")
         for u in range(2):
             for b in range(PASSES):
-                rounded_act["q", b, u] = q_bf[:, u, PACK * half * b : PACK * half * (b + 1)]
+                act_bf["q", b, u] = q_bf[:, u, PACK * HALF * b : PACK * HALF * (b + 1)]
         for b in range(PASSES):
-            rectify_half("q", b, 0)
+            rectify("q", b, 0)
         prepare_w1(1, 0, P)
         quantize_q(0, "w1_raw10")
         for b in range(PASSES):
-            rectify_half("q", b, 1)
+            rectify("q", b, 1)
+
+        head_acc, head_sb = {}, {}
+
+        def head_part(u, t):
+            return head_acc[u, t // 2][:, HALF * (t % 2) : HALF * (t % 2 + 1)]
+
+        def start_head(u, number):
+            for g in range(2):
+                head_acc[u, g] = bank("head_acc", number + g)
+            for t in range(PACK):
+                second_q(head_part(u, t), 0, t, u, t % 2 == 0)
+
+        def finish_head(u):
+            for a in range(PASSES):
+                for t in range(PACK):
+                    second_p(head_part(u, t), a, 0, t, u, a == PASSES - 1 and t % 2 == 1)
+
+        def empty_head(u, g, on=None):
+            head_sb[u, g] = held("head_sb%d%d" % (u, g), [P, 2, HALF], F32, on)
+            nc.scalar.copy(head_sb[u, g][:].rearrange("p t j -> p (t j)"), head_acc[u, g][:])
+
+        def scatter(a, t, src, lo, hi):
+            nc.vector.tensor_tensor(
+                page[a, t][:].indirect(idx3[:, lo // LANES : hi // LANES]), src, gain[t][:, lo:hi], MULT
+            )
 
         open_first("p", 0, 0, 0)
         for a in range(PASSES):
             first_stage("p", a, 0, 0)
         prepare_w1(0, 1, P)
         open_p(0, 0)
-        rectify_half("p", 0, 0)
-        head_acc = {(0, g): bank("head_acc", 4 + g) for g in range(2)}
-        for t in range(PACK):
-            second_q(head_acc[0, t // 2][:, half * (t % 2) : half * (t % 2 + 1)], 0, t, 0, t % 2 == 0)
+        rectify("p", 0, 0)
+        start_head(0, 4)
         open_first("p", 1, 0, 2)
         first_stage("p", 0, 1, 0)
-        prepare_w1(1, 1, 88)
+        prepare_w1(1, 1, LAST_SHARE)
         first_stage("p", 1, 1, 0)
         quantize_p(0, 0, "w1_raw11")
         quantize_q(1, "p_bf00")
         open_p(1, 0)
-        rectify_half("p", 1, 0, (1,))
+        rectify("p", 1, 0, vector_chunks=(1,))
         quantize_p(1, 0)
         v2_scale = held("v2_scale", [P, S2], U8, "p_bf10")
         nc.vector.tensor_copy(v2_scale[:], tab2_scale[:].indirect(idx2[:]))
-
-        head_sb = {}
-
-        def finish_head(u):
-            for a in range(PASSES):
-                for t in range(PACK):
-                    second_p(head_acc[u, t // 2][:, half * (t % 2) : half * (t % 2 + 1)], a, 0, t, u,
-                             a == PASSES - 1 and t % 2 == 1)
-
-        def empty_head(u, g, on=None):
-            head_sb[u, g] = held("head_sb%d%d" % (u, g), [P, 2, half], F32, on)
-            nc.scalar.copy(head_sb[u, g][:].rearrange("p t j -> p (t j)"), head_acc[u, g][:])
-
-        def scatter(a, t, src, lo, hi):
-            nc.vector.tensor_tensor(
-                page[a, t][:].indirect(idx3[:, lo // 16 : hi // 16]), src, gain[t][:, lo:hi], MULT
-            )
-
         finish_head(0)
         empty_head(0, 0)
 
@@ -310,24 +314,22 @@ def tile_list_binning_order_scores_kernel(
             for a in range(PASSES):
                 first_stage("p", a, b, 1)
             open_p(b, 1)
-            rectify_half("p", b, 1)
-        for t in range(2):
-            scatter(0, t, head_sb[0, 0][:, t, :], 0, half)
+            rectify("p", b, 1)
+        for t in (0, 1):
+            scatter(0, t, head_sb[0, 0][:, t, :], 0, HALF)
         for b in (1, 0):
             quantize_p(b, 1)
         empty_head(0, 1, "p_bf11")
-        v2_code = [held("v2_code0", [P, S2], I32, "p_bf01"), None]
+        v2_code = {}
 
-        def gather_tab2(a):
+        def gather_tab2(a, on):
+            v2_code[a] = held("v2_code%d" % a, [P, S2], I32, on)
             nc.vector.tensor_copy(v2_code[a][:].bitcast(U32), tab2_word[a][:].bitcast(U32).indirect(idx2[:]))
 
-        gather_tab2(0)
-        for t in range(2, PACK):
-            scatter(0, t, head_sb[0, 1][:, t % 2, :], 0, half)
-        for g in range(2):
-            head_acc[1, g] = bank("head_acc", g)
-        for t in range(PACK):
-            second_q(head_acc[1, t // 2][:, half * (t % 2) : half * (t % 2 + 1)], 0, t, 1, t % 2 == 0)
+        gather_tab2(0, "p_bf01")
+        for t in (2, 3):
+            scatter(0, t, head_sb[0, 1][:, t % 2, :], 0, HALF)
+        start_head(1, 0)
         finish_head(1)
         for g in range(2):
             empty_head(1, g)
@@ -338,82 +340,101 @@ def tile_list_binning_order_scores_kernel(
             h_sb[t] = held("h_sb%d" % t, [P, S], F32, on)
             nc.scalar.copy(h_sb[t][:], h_acc[t][:])
 
-        for n, t in enumerate(last_order):
-            h_acc[t] = bank("h_acc", 4 + n)
+        for place, t in enumerate(LAST_ORDER):
+            h_acc[t] = bank("h_acc", 4 + place)
             for u in range(2):
-                second_q(h_acc[t][:, half * u : half * (u + 1)], 1, t, u, u == 0)
+                second_q(h_acc[t][:, HALF * u : HALF * (u + 1)], 1, t, u, u == 0)
             for u in range(2):
                 for a in range(PASSES):
-                    second_p(h_acc[t][:, half * u : half * (u + 1)], a, 1, t, u, u == 1 and a == PASSES - 1)
-            if t != 3:
+                    second_p(h_acc[t][:, HALF * u : HALF * (u + 1)], a, 1, t, u, u == 1 and a == PASSES - 1)
+            if t != LAST_ORDER[-1]:
                 empty_h(t)
 
-        pairs = {(a, u): held("pairs%d%d" % (a, u), [P, 2, BANK, 2], BF16, "w1_bf%d%d" % (a, u))
-                 for a in range(PASSES) for u in range(2)}
+        pairs = {(a, w): held("pairs%d%d" % (a, w), [P, 2, BANK, 2], BF16, "w1_bf%d%d" % (a, w))
+                 for a in range(PASSES) for w in range(2)}
         woven = [held("woven0", [P, PACK * T2], BF16, "w1_raw01"), held("woven1", [P, PACK * T2], BF16, "w1_raw10")]
         page_code = [held("page_code%d" % a, [P, T2], I32) for a in range(PASSES)]
-        page_scale = [None, held("page_scale1", [P, T2], U8)]
-        rows = S2 // P
+        page_scale = {1: held("page_scale1", [P, T2], U8)}
 
-        for i in range(rows):
+        for i in range(OUT_TILES):
             nc.scalar.activation(prior[:, i, :], prior[:, i, :], COPY, scale=blend[:, i : i + 1])
 
-        def round_in(a, t, u, copy):
-            copy(pairs[a, u][:, t // 2, :, t % 2], page[a, t][:, BANK * u : BANK * (u + 1)])
+        def round_in(a, t, w, copy, lo=0, hi=BANK):
+            copy(pairs[a, w][:, t // 2, lo:hi, t % 2], page[a, t][:, BANK * w + lo : BANK * w + hi])
 
-        def weave(a, u, copy):
-            words = pairs[a, u][:].rearrange("p g c e -> p g (c e)").bitcast(F32)
-            dst = woven[a][:, PACK * BANK * u : PACK * BANK * (u + 1)].bitcast(F32)
+        def weave(a, w, copy):
+            words = pairs[a, w][:].rearrange("p g c e -> p g (c e)").bitcast(F32)
+            dst = woven[a][:, PACK * BANK * w : PACK * BANK * (w + 1)].bitcast(F32)
             copy(dst.rearrange("p (c g) -> p c g", g=2), words.rearrange("p g c -> p c g"))
 
         for t in range(PACK):
-            scatter(0, t, head_sb[1, t // 2][:, t % 2, :], half, S)
-            for u in range(2):
-                round_in(0, t, u, nc.scalar.copy)
-        for u in range(2):
-            weave(0, u, nc.scalar.copy)
-
-        v2_code[1] = held("v2_code1", [P, S2], I32, "head_sb11")
-        gather_tab2(1)
+            scatter(0, t, head_sb[1, t // 2][:, t % 2, :], HALF, S)
+            for w in range(2):
+                round_in(0, t, w, nc.scalar.copy)
+        for w in range(2):
+            weave(0, w, nc.scalar.copy)
+        gather_tab2(1, "head_sb11")
 
         e_acc = {}
 
-        def score_pass(a, i, u):
-            side = (v2_code[a][:, P * i : P * (i + 1)].bitcast(FP8X4), v2_scale[4 * a :, P * i : P * (i + 1)])
-            mx(e_acc[i, u][:], side, page_code[a], page_scale[a], slice(BANK * u, BANK * (u + 1)), a == 0, a == 1)
+        def spans(i, w):
+            if i == 0:
+                return [(0, BANK * w, BANK)]
+            if w == 0:
+                return [(0, QUARTER, BANK)]
+            return [(QUARTER, 3 * QUARTER, QUARTER), (0, 0, QUARTER)]
 
-        for t in last_order[:3]:
+        def score_pass(a, i, w):
+            stationary = (
+                v2_code[a][:, P * i : P * (i + 1)].bitcast(FP8X4),
+                v2_scale[SCALE_ROWS * a :, P * i : P * (i + 1)],
+            )
+            parts = spans(i, w)
+            for place, (at, lo, width) in enumerate(parts):
+                mx(e_acc[i, w][:, at : at + width], stationary, page_code[a], page_scale[a], slice(lo, lo + width),
+                   a == 0 and place == 0, a == PASSES - 1 and place == len(parts) - 1)
+
+        for t in LAST_ORDER[:-1]:
             scatter(1, t, h_sb[t][:], 0, S)
-            for u in range(2):
-                round_in(1, t, u, nc.scalar.copy)
-            if t == 2:
-                empty_h(3, "page12")
+            for w in range(2):
+                round_in(1, t, w, nc.scalar.copy)
+            if t == LAST_ORDER[0]:
+                empty_h(LAST_ORDER[-1], "page12")
         page_scale[0] = held("page_scale0", [P, T2], U8, "h_sb1")
         quantize(page_code[0], page_scale[0], woven[0], 0, T2)
-        for u in range(2):
-            for i in range(rows):
-                e_acc[i, u] = bank("e_acc", 4 * u + i)
-                score_pass(0, i, u)
+        for w in range(2):
+            for i in range(OUT_TILES):
+                e_acc[i, w] = bank("e_acc", OUT_TILES * w + i)
+                score_pass(0, i, w)
         scatter(1, 3, h_sb[3][:], 0, S)
 
-        for u, copy in ((0, nc.vector.tensor_copy), (1, nc.scalar.copy)):
-            round_in(1, 3, u, copy)
-            weave(1, u, copy)
-        for u in range(2):
-            quantize(page_code[1], page_scale[1], woven[1], BANK * u, BANK * (u + 1))
-            for i in range(rows):
-                score_pass(1, i, u)
+        round_in(1, 3, 0, nc.vector.tensor_copy)
+        round_in(1, 3, 1, nc.vector.tensor_copy, 0, QUARTER)
+        round_in(1, 3, 1, nc.scalar.copy, QUARTER, BANK)
+        weave(1, 0, nc.vector.tensor_copy)
+        weave(1, 1, nc.scalar.copy)
+        for w in range(2):
+            quantize(page_code[1], page_scale[1], woven[1], BANK * w, BANK * (w + 1))
 
-        e_sb = [held("e_sb%d" % i, [P, T2], F32, "page0%d" % i) for i in range(rows)]
-        for i in range(rows):
-            for u in range(2):
-                copy = nc.vector.tensor_copy if (i, u) == (1, 0) else nc.scalar.copy
-                copy(e_sb[i][:, BANK * u : BANK * (u + 1)], e_acc[i, u][:])
-        for i in range(rows):
+        e_sb = [held("e_sb%d" % i, [P, T2], F32, "page0%d" % i) for i in range(OUT_TILES)]
+        for i in range(OUT_TILES):
+            for w in range(2):
+                score_pass(1, i, w)
+            if i == 0:
+                for w in range(2):
+                    nc.scalar.copy(e_sb[i][:, BANK * w : BANK * (w + 1)], e_acc[i, w][:])
+            else:
+                nc.scalar.copy(e_sb[i][:, QUARTER : 3 * QUARTER], e_acc[i, 0][:])
+                nc.scalar.copy(
+                    e_sb[i][:].rearrange("p (x c) -> p x c", c=QUARTER)[:, 0:4:3, :],
+                    e_acc[i, 1][:].rearrange("p (x c) -> p x c", c=QUARTER),
+                )
+
+        for i in range(OUT_TILES):
             res = held("res%d" % i, [P, PICK], F32)
-            pieces = ((0, PICK),) if i < rows - 1 else ((0, PICK // 2), (PICK // 2, PICK))
+            pieces = ((0, PICK),) if i < OUT_TILES - 1 else ((0, PICK // 2), (PICK // 2, PICK))
             for lo, hi in pieces:
                 nc.vector.tensor_tensor(
-                    res[:, lo:hi], e_sb[i][:].indirect(idx4[:, lo // 16 : hi // 16]), prior[:, i, lo:hi], ADD
+                    res[:, lo:hi], e_sb[i][:].indirect(idx4[:, lo // LANES : hi // LANES]), prior[:, i, lo:hi], ADD
                 )
                 nc.sync.dma_start(out[P * i : P * (i + 1), lo:hi], res[:, lo:hi])

from contextlib import ExitStack

import concourse.mybir as mybir
from concourse.masks import make_identity

K, T, S, T2, T3, S2, PICK = 1024, 2048, 512, 1024, 2048, 512, 512
FLOPS = 4 * 2 * K * K * S + 2 * K * S2 * T2

F32 = mybir.dt.float32
BF16 = mybir.dt.bfloat16
I32 = mybir.dt.int32
U32 = mybir.dt.uint32
U16 = mybir.dt.uint16
U8 = mybir.dt.uint8
FP8X4 = mybir.dt.float8_e4m3fn_x4
FP4X4 = mybir.dt.float4_e2m1fn_x4
MULT = mybir.AluOpType.mult
ADD = mybir.AluOpType.add
MAX = mybir.AluOpType.max
RELU = mybir.ActivationFunctionType.Relu
COPY = mybir.ActivationFunctionType.Copy

P = 128
PACK = 4
PASS = P * PACK
PASSES = K // PASS
QUADS = 4
QUAD = P // QUADS
SCALE_ROWS = 4
LANES = 16
BANK = 512
CHUNK = 128
HALF = S // 2
QUARTER = T2 // 4
OUT_TILES = S2 // P
ALIGN = 64
FIRST_SHARE, LAST_SHARE = 96, 88
LAST_ORDER = (2, 0, 1, 3)


def tile_list_binning_order_scores_kernel(
    tc, tab_words, tab_scales, offs, w1, w4_words, w4_scales, page0, wgs, offs3,
    tab2_words, tab2_scales, offs2, offs4, be, ref, out,
):
    nc = tc.nc
    with ExitStack() as ctx:
        lists = ctx.enter_context(tc.tile_pool(name="lists", bufs=1))
        keep = ctx.enter_context(tc.tile_pool(name="keep", bufs=1))
        psum = ctx.enter_context(tc.psum_pool(name="psum", bufs=1))

        def held(name, shape, dtype, on=None):
            return keep.tile(shape, dtype, name=name, tag=on or name, align_bytes=ALIGN)

        def bank(name, number):
            return psum.tile([P, BANK], F32, name=name, tag="bank%d" % number)

        idx = lists.tile([P, S // LANES], U16, name="idx")
        idx2 = lists.tile([P, S2 // LANES], U16, name="idx2")
        idx3 = lists.tile([P, S // LANES], U16, name="idx3")
        idx4 = lists.tile([P, PICK // LANES], U16, name="idx4")

        w4_scale_raw = held("w4_scale_raw", [P, PASSES, K], U8)
        tab_scale = held("tab_scale", [P, PASSES, T], U8)
        tab2_scale = held("tab2_scale", [P, T3], U8)
        nc.vector.memset(tab_scale[:, 0, :].bitcast(I32), 0)
        nc.gpsimd.memset(tab_scale[:, 1, :].bitcast(I32), 0)
        nc.vector.memset(w4_scale_raw[:].rearrange("p a c -> p (a c)").bitcast(I32), 0)
        nc.vector.memset(tab2_scale[:].bitcast(I32), 0)

        identity = held("identity", [P, P], F32)
        make_identity(nc, identity[:])
        wgs_raw = held("wgs_raw", [P, S], F32)
        nc.sync.dma_start(wgs_raw[:], wgs)
        w4_raw = held("w4_raw", [P, PASSES, K // 2], I32)
        tab_word = [held("tab_word%d" % a, [P, T], I32) for a in range(PASSES)]
        nc.sync.dma_start(w4_raw[:], w4_words.bitcast(I32).rearrange("a p w -> p a w"))
        nc.sync.dma_start(idx[:], offs)

        def load_scales(tile, scale_rows):
            for r in range(SCALE_ROWS):
                nc.sync.dma_start(
                    tile[r:P:QUAD].bitcast(I32),
                    scale_rows.bitcast(I32).rearrange("a (q r) w -> r q a w", r=SCALE_ROWS)[r],
                )

        load_scales(tab_scale, tab_scales)
        nc.sync.dma_start(tab_word[0][:], tab_words[0].rearrange("p n i -> p (n i)").bitcast(I32))
        load_scales(w4_scale_raw, w4_scales)
        nc.sync.dma_start(tab_word[1][:], tab_words[1].rearrange("p n i -> p (n i)").bitcast(I32))

        w1_raw = {}
        for b in range(PASSES):
            for a in range(PASSES):
                w1_raw[a, b] = held("w1_raw%d%d" % (a, b), [P, PACK, PASS], F32)
                nc.sync.dma_start(
                    w1_raw[a, b][:],
                    w1[PASS * a : PASS * (a + 1), PASS * b : PASS * (b + 1)].rearrange("(p i) c -> p i c", i=PACK),
                )
                if (a, b) == (0, 0):
                    nc.sync.dma_start(idx2[:], offs2)
                    nc.sync.dma_start(idx3[:], offs3)

        page = {(a, t): held("page%d%d" % (a, t), [P, T2], F32) for a in range(PASSES) for t in range(PACK)}
        page_rows = page0.rearrange("(a p t) c -> a t p c", a=PASSES, t=PACK)
        tab2_word = [held("tab2_word%d" % a, [P, T3], I32) for a in range(PASSES)]
        blend = held("blend", [P, OUT_TILES], F32)
        prior = held("prior", [P, OUT_TILES, PICK], F32)

        def load_tab2(a):
            nc.sync.dma_start(tab2_word[a][:], tab2_words[a].rearrange("p n i -> p (n i)").bitcast(I32))

        for quad in (0, 2, 1, 3):
            nc.sync.dma_start(
                tab2_scale[QUAD * quad : QUAD * quad + PASSES * SCALE_ROWS].bitcast(I32),
                tab2_scales[:, SCALE_ROWS * quad : SCALE_ROWS * (quad + 1), :].bitcast(I32),
            )
        for t in (0, 1):
            nc.sync.dma_start(page[0, t][:], page_rows[0, t])
        load_tab2(0)
        for t in (2, 3):
            nc.sync.dma_start(page[0, t][:], page_rows[0, t])
        nc.sync.dma_start(idx4[:], offs4)
        with nc.allow_non_contiguous_dma(reason="one weight to a partition"):
            nc.sync.dma_start(blend[:], be.rearrange("(i p) -> p i", p=P))
        nc.sync.dma_start(prior[:], ref.rearrange("(i p) m -> p i m", p=P))
        load_tab2(1)
        for t in LAST_ORDER:
            nc.sync.dma_start(page[1, t][:], page_rows[1, t])

        turned = bank("turned", 4)
        for blk in range(S // P):
            nc.tensor.transpose(turned[:, P * blk : P * (blk + 1)], wgs_raw[:, P * blk : P * (blk + 1)], identity[:])
        spread = held("spread", [P, S // P, PACK, QUADS, QUAD], F32)
        for quad in range(QUADS):
            nc.scalar.copy(
                spread[:, :, :, quad, :], turned[:].rearrange("p (blk m t) -> p blk t m", blk=S // P, t=PACK)
            )
        gain = [held("gain%d" % t, [P, S], F32) for t in range(PACK)]
        for t in range(PACK):
            back = bank("back", t)
            for blk in range(S // P):
                nc.tensor.transpose(
                    back[:, P * blk : P * (blk + 1)], spread[:, blk, t].rearrange("p q m -> p (q m)"), identity[:]
                )
            nc.scalar.copy(gain[t][:], back[:])

        w4_code = [held("w4_code%d" % a, [P, 2 * K], U8) for a in range(PASSES)]
        w4_scale = [held("w4_scale0", [P, K], U8, "spread"), held("w4_scale1", [P, K], U8)]
        v_code = [held("v_code%d" % a, [P, S], I32) for a in range(PASSES)]
        v_scale = [held("v_scale%d" % a, [P, S], U8) for a in range(PASSES)]

        def sort_columns(dst, src):
            nc.vector.tensor_copy(
                dst.rearrange("p (b t m) -> p b t m", b=PASSES, t=PACK),
                src.rearrange("p (b m t) -> p b t m", b=PASSES, t=PACK),
            )

        for a in range(PASSES):
            sort_columns(w4_code[a][:].bitcast(U16), w4_raw[:, a, :].bitcast(U16))
            nc.vector.tensor_copy(v_code[a][:].bitcast(U32), tab_word[a][:].bitcast(U32).indirect(idx[:]))
            sort_columns(w4_scale[a][:], w4_scale_raw[:, a, :])
            nc.vector.tensor_copy(v_scale[a][:], tab_scale[:, a, :].indirect(idx[:]))

        w1_code, w1_scale = {}, {}

        def w4_columns(a, b, t):
            col = PASS * b + P * t
            return w4_code[a][:, 2 * col : 2 * (col + P)].bitcast(FP4X4), w4_scale[a][:, col : col + P]

        def w1_columns(a, b, t):
            col = P * t
            return w1_code[a, b][:, col : col + P].bitcast(FP8X4), w1_scale[a, b][:, col : col + P]

        def mx(acc, stationary, code, scale, cols, start, stop):
            nc.tensor.matmul_mx(
                out=acc, lhsT=stationary[0], lhsT_scale=stationary[1],
                rhs=code[:, cols].bitcast(FP8X4), rhs_scale=scale[:, cols], start=start, stop=stop,
            )

        def quantize(code, scale, src, lo, hi):
            nc.vector.quantize_mx(code[:, lo:hi].bitcast(FP8X4), scale[:, lo:hi], src[:, PACK * lo : PACK * hi])

        def prepare_w1(a, b, share):
            rounded = held("w1_bf%d%d" % (a, b), [P, PACK * PASS], BF16)
            dst = rounded[:].rearrange("p (t m i) -> p m t i", t=PACK, i=PACK)
            src = w1_raw[a, b][:].rearrange("p i (m t) -> p m t i", t=PACK)
            nc.vector.tensor_scalar(dst[:, :share], src[:, :share], -1.0, None, MULT)
            if share < P:
                nc.scalar.activation(dst[:, share:], src[:, share:], COPY, scale=-1.0)
            w1_code[a, b] = held("w1_code%d%d" % (a, b), [P, PASS], I32)
            w1_scale[a, b] = held("w1_scale%d%d" % (a, b), [P, PASS], U8)
            quantize(w1_code[a, b], w1_scale[a, b], rounded, 0, PASS)

        act_bf, act_code, act_scale, first_acc = {}, {}, {}, {}

        def open_first(name, b, u, number):
            for c in range(2):
                first_acc[name, b, 2 * u + c] = bank(name + "_acc", number + c)

        def first_stage(name, a, b, u):
            columns = w4_columns if name == "q" else w1_columns
            for chunk in (2 * u, 2 * u + 1):
                for t in range(PACK):
                    mx(first_acc[name, b, chunk][:, CHUNK * t : CHUNK * (t + 1)], columns(a, b, t),
                       v_code[a], v_scale[a], slice(CHUNK * chunk, CHUNK * (chunk + 1)),
                       a == 0 and t == 0, a == PASSES - 1 and t == PACK - 1)

        def rectify(name, b, u, vector_chunks=()):
            sign = 1.0 if name == "q" else -1.0
            for c in range(2):
                dst = act_bf[name, b, u][:, PACK * CHUNK * c : PACK * CHUNK * (c + 1)]
                dst = dst.rearrange("p (n t) -> p n t", t=PACK)
                src = first_acc[name, b, 2 * u + c][:].rearrange("p (t n) -> p n t", t=PACK)
                if c in vector_chunks:
                    nc.vector.tensor_scalar(dst, src, sign, 0.0, MULT, MAX)
                else:
                    nc.scalar.activation(dst, src, RELU, scale=sign)

        def open_p(b, u):
            act_bf["p", b, u] = held("p_bf%d%d" % (b, u), [P, PACK * HALF], BF16)

        def quantize_p(b, u, on=None):
            act_code["p", b, u] = held("p_code%d%d" % (b, u), [P, HALF], I32)
            act_scale["p", b, u] = held("p_scale%d%d" % (b, u), [P, HALF], U8, on)
            quantize(act_code["p", b, u], act_scale["p", b, u], act_bf["p", b, u], 0, HALF)

        def quantize_q(u, on):
            code = held("q_code%d" % u, [P, PASSES * HALF], I32)
            scale = held("q_scale%d" % u, [P, PASSES * HALF], U8, on)
            quantize(code, scale, q_bf[:, u, :], 0, PASSES * HALF)
            for b in range(PASSES):
                act_code["q", b, u] = code[:, HALF * b : HALF * (b + 1)]
                act_scale["q", b, u] = scale[:, HALF * b : HALF * (b + 1)]

        def second_q(acc, b, t, u, start):
            for a in range(PASSES):
                mx(acc, w1_columns(a, b, t), act_code["q", a, u], act_scale["q", a, u], slice(0, HALF),
                   start and a == 0, False)

        def second_p(acc, a, b, t, u, stop):
            for c in range(2):
                cols = slice(CHUNK * c, CHUNK * (c + 1))
                mx(acc[:, cols], w4_columns(a, b, t), act_code["p", a, u], act_scale["p", a, u], cols,
                   False, stop and c == 1)

        for u in range(2):
            for b in range(PASSES):
                open_first("q", b, u, 4 * u + 2 * b)
        for a in range(PASSES):
            for u in range(2):
                for b in range(PASSES):
                    first_stage("q", a, b, u)
        prepare_w1(0, 0, FIRST_SHARE)
        q_bf = held("q_bf", [P, 2, PASSES * PACK * HALF], BF16, "w1_raw00")
        for u in range(2):
            for b in range(PASSES):
                act_bf["q", b, u] = q_bf[:, u, PACK * HALF * b : PACK * HALF * (b + 1)]
        for b in range(PASSES):
            rectify("q", b, 0)
        prepare_w1(1, 0, P)
        quantize_q(0, "w1_raw10")
        for b in range(PASSES):
            rectify("q", b, 1)

        head_acc, head_sb = {}, {}

        def head_part(u, t):
            return head_acc[u, t // 2][:, HALF * (t % 2) : HALF * (t % 2 + 1)]

        def start_head(u, number):
            for g in range(2):
                head_acc[u, g] = bank("head_acc", number + g)
            for t in range(PACK):
                second_q(head_part(u, t), 0, t, u, t % 2 == 0)

        def finish_head(u):
            for a in range(PASSES):
                for t in range(PACK):
                    second_p(head_part(u, t), a, 0, t, u, a == PASSES - 1 and t % 2 == 1)

        def empty_head(u, g, on=None):
            head_sb[u, g] = held("head_sb%d%d" % (u, g), [P, 2, HALF], F32, on)
            nc.scalar.copy(head_sb[u, g][:].rearrange("p t j -> p (t j)"), head_acc[u, g][:])

        def scatter(a, t, src, lo, hi):
            nc.vector.tensor_tensor(
                page[a, t][:].indirect(idx3[:, lo // LANES : hi // LANES]), src, gain[t][:, lo:hi], MULT
            )

        open_first("p", 0, 0, 0)
        for a in range(PASSES):
            first_stage("p", a, 0, 0)
        prepare_w1(0, 1, P)
        open_p(0, 0)
        rectify("p", 0, 0)
        start_head(0, 4)
        open_first("p", 1, 0, 2)
        first_stage("p", 0, 1, 0)
        prepare_w1(1, 1, LAST_SHARE)
        first_stage("p", 1, 1, 0)
        quantize_p(0, 0, "w1_raw11")
        quantize_q(1, "p_bf00")
        open_p(1, 0)
        rectify("p", 1, 0, vector_chunks=(1,))
        quantize_p(1, 0)
        v2_scale = held("v2_scale", [P, S2], U8, "p_bf10")
        nc.vector.tensor_copy(v2_scale[:], tab2_scale[:].indirect(idx2[:]))
        finish_head(0)
        empty_head(0, 0)

        open_first("p", 1, 1, 6)
        open_first("p", 0, 1, 2)
        for b in (1, 0):
            for a in range(PASSES):
                first_stage("p", a, b, 1)
            open_p(b, 1)
            rectify("p", b, 1)
        for t in (0, 1):
            scatter(0, t, head_sb[0, 0][:, t, :], 0, HALF)
        for b in (1, 0):
            quantize_p(b, 1)
        empty_head(0, 1, "p_bf11")
        v2_code = {}

        def gather_tab2(a, on):
            v2_code[a] = held("v2_code%d" % a, [P, S2], I32, on)
            nc.vector.tensor_copy(v2_code[a][:].bitcast(U32), tab2_word[a][:].bitcast(U32).indirect(idx2[:]))

        gather_tab2(0, "p_bf01")
        for t in (2, 3):
            scatter(0, t, head_sb[0, 1][:, t % 2, :], 0, HALF)
        start_head(1, 0)
        finish_head(1)
        for g in range(2):
            empty_head(1, g)

        h_acc, h_sb = {}, {}

        def empty_h(t, on=None):
            h_sb[t] = held("h_sb%d" % t, [P, S], F32, on)
            nc.scalar.copy(h_sb[t][:], h_acc[t][:])

        for place, t in enumerate(LAST_ORDER):
            h_acc[t] = bank("h_acc", 4 + place)
            for u in range(2):
                second_q(h_acc[t][:, HALF * u : HALF * (u + 1)], 1, t, u, u == 0)
            for u in range(2):
                for a in range(PASSES):
                    second_p(h_acc[t][:, HALF * u : HALF * (u + 1)], a, 1, t, u, u == 1 and a == PASSES - 1)
            if t != LAST_ORDER[-1]:
                empty_h(t)

        pairs = {(a, w): held("pairs%d%d" % (a, w), [P, 2, BANK, 2], BF16, "w1_bf%d%d" % (a, w))
                 for a in range(PASSES) for w in range(2)}
        woven = [held("woven0", [P, PACK * T2], BF16, "w1_raw01"), held("woven1", [P, PACK * T2], BF16, "w1_raw10")]
        page_code = [held("page_code%d" % a, [P, T2], I32) for a in range(PASSES)]
        page_scale = {1: held("page_scale1", [P, T2], U8)}

        for i in range(OUT_TILES):
            nc.scalar.activation(prior[:, i, :], prior[:, i, :], COPY, scale=blend[:, i : i + 1])

        def round_in(a, t, w, copy, lo=0, hi=BANK):
            copy(pairs[a, w][:, t // 2, lo:hi, t % 2], page[a, t][:, BANK * w + lo : BANK * w + hi])

        def weave(a, w, copy):
            words = pairs[a, w][:].rearrange("p g c e -> p g (c e)").bitcast(F32)
            dst = woven[a][:, PACK * BANK * w : PACK * BANK * (w + 1)].bitcast(F32)
            copy(dst.rearrange("p (c g) -> p c g", g=2), words.rearrange("p g c -> p c g"))

        for t in range(PACK):
            scatter(0, t, head_sb[1, t // 2][:, t % 2, :], HALF, S)
            for w in range(2):
                round_in(0, t, w, nc.scalar.copy)
        for w in range(2):
            weave(0, w, nc.scalar.copy)
        gather_tab2(1, "head_sb11")

        e_acc = {}

        def spans(i, w):
            if i == 0:
                return [(0, BANK * w, BANK)]
            if w == 0:
                return [(0, QUARTER, BANK)]
            return [(QUARTER, 3 * QUARTER, QUARTER), (0, 0, QUARTER)]

        def score_pass(a, i, w):
            stationary = (
                v2_code[a][:, P * i : P * (i + 1)].bitcast(FP8X4),
                v2_scale[SCALE_ROWS * a :, P * i : P * (i + 1)],
            )
            parts = spans(i, w)
            for place, (at, lo, width) in enumerate(parts):
                mx(e_acc[i, w][:, at : at + width], stationary, page_code[a], page_scale[a], slice(lo, lo + width),
                   a == 0 and place == 0, a == PASSES - 1 and place == len(parts) - 1)

        for t in LAST_ORDER[:-1]:
            scatter(1, t, h_sb[t][:], 0, S)
            for w in range(2):
                round_in(1, t, w, nc.scalar.copy)
            if t == LAST_ORDER[0]:
                empty_h(LAST_ORDER[-1], "page12")
        page_scale[0] = held("page_scale0", [P, T2], U8, "h_sb1")
        quantize(page_code[0], page_scale[0], woven[0], 0, T2)
        for w in range(2):
            for i in range(OUT_TILES):
                e_acc[i, w] = bank("e_acc", OUT_TILES * w + i)
                score_pass(0, i, w)
        scatter(1, 3, h_sb[3][:], 0, S)

        round_in(1, 3, 0, nc.vector.tensor_copy)
        round_in(1, 3, 1, nc.vector.tensor_copy, 0, QUARTER)
        round_in(1, 3, 1, nc.scalar.copy, QUARTER, BANK)
        weave(1, 0, nc.vector.tensor_copy)
        weave(1, 1, nc.scalar.copy)
        for w in range(2):
            quantize(page_code[1], page_scale[1], woven[1], BANK * w, BANK * (w + 1))

        e_sb = [held("e_sb%d" % i, [P, T2], F32, "page0%d" % i) for i in range(OUT_TILES)]
        for i in range(OUT_TILES):
            for w in range(2):
                score_pass(1, i, w)
            if i == 0:
                for w in range(2):
                    nc.scalar.copy(e_sb[i][:, BANK * w : BANK * (w + 1)], e_acc[i, w][:])
            else:
                nc.scalar.copy(e_sb[i][:, QUARTER : 3 * QUARTER], e_acc[i, 0][:])
                nc.scalar.copy(
                    e_sb[i][:].rearrange("p (x c) -> p x c", c=QUARTER)[:, 0:4:3, :],
                    e_acc[i, 1][:].rearrange("p (x c) -> p x c", c=QUARTER),
                )

        for i in range(OUT_TILES):
            res = held("res%d" % i, [P, PICK], F32)
            pieces = ((0, PICK),) if i < OUT_TILES - 1 else ((0, PICK // 2), (PICK // 2, PICK))
            for lo, hi in pieces:
                nc.vector.tensor_tensor(
                    res[:, lo:hi], e_sb[i][:].indirect(idx4[:, lo // LANES : hi // LANES]), prior[:, i, lo:hi], ADD
                )
                nc.sync.dma_start(out[P * i : P * (i + 1), lo:hi], res[:, lo:hi])
